import numpy as np, ml_dtypes
CORES = [2,6,10,14,18,22,26,30]
N = 8
import mx_ref
BF = ml_dtypes.bfloat16
def pick(q, e):
    c = np.concatenate([q[0].reshape(128, -1, 4), np.zeros((128, 1, 4), np.uint8)], axis=1); s = np.concatenate([q[1], np.ones((16, 1), np.uint8)], axis=1)
    return (np.ascontiguousarray(c[:, e].reshape(128, -1)), np.ascontiguousarray(s[:, e]))
def join(*qs):
    return (np.concatenate([q[0] for q in qs], axis=1), np.concatenate([q[1] for q in qs], axis=1))
def put(q, e, v):
    c, s = q[0].reshape(128, -1, 4).copy(), q[1].copy(); c[:, e] = v[0].reshape(128, -1, 4); s[:, e] = v[1]
    return (c.reshape(128, -1), s)
def pk(c, s):
    return (np.ascontiguousarray(c), mx_ref.live(s))
def emit(q):
    return q[0], q[1]
def decode(q):
    o = []
    for b in range(4):
        e = np.zeros((128, 128, 4), np.float32); e[np.arange(128), np.arange(128), b] = 1
        o.append(mx_ref.matmul(mx_ref.quantize(e.reshape(128, 512).astype(BF)), q))
    return np.stack(o, axis=2).reshape(128, -1)
def cut(t, i, w=512):
    return t[:, w * i:w * i + w]
def f(rng, *shape):
    return mx_ref.flush((rng.standard_normal(shape, dtype=np.float32) * np.exp2(rng.integers(-2, 3, shape[:-1] + (1,)))).astype(BF))
def wide(rng, *shape, cols=0):
    v = rng.standard_normal(shape, dtype=np.float32) * np.exp2(rng.integers(-12, 13, shape)).astype(np.float32)
    if cols: v *= np.repeat(np.exp2(rng.integers(-cols, cols + 1, shape[:-2] + (1, shape[-1] // 4))) * (rng.random(shape[:-2] + (1, shape[-1] // 4)) > 0.0625), 4, axis=-1).astype(np.float32)
    return mx_ref.flush(v.astype(BF))
P, K, R, O = 256, 48, 3, 1
def big(v):
    v = v.astype(np.float32)
    v[np.abs(v) < np.float32(2.0 ** -16)] = 0
    return v.astype(BF)
def plain(rng):
    u = np.array(f(rng, N, 128, 512))
    u[:, :, 4 * R:] = 0
    return {"c": big(f(rng, N, 128, 4 * P)), "u": u, "w": f(rng, N, 128, 512 * O)}
def bf(v, *shape):
    return np.ascontiguousarray(v).reshape(shape).astype(np.float32).astype(BF)
def signs(rng):
    return rng.choice([-1.0, 1.0], (128, 1, 4))
def heavy(rng, way):
    d, g = plain(rng), signs(rng)
    size = np.exp2(rng.integers(0, 3, (N, P)))
    size[np.arange(N), rng.integers(0, P, N)] = 1024
    d["c"] = bf((1 + rng.random((N, 128, P, 4))) * size[:, None, :, None] * g * 2.0 ** 18, N, 128, 4 * P)
    d["u"][:, :, :4 * R] = bf((1 + rng.random((N, 128, R, 4))) * g * np.asarray(way)[:, None] * 2.0 ** 28, N, 128, 4 * R)
    return d
def setup_inputs(rng):
    return plain(rng)
def setup_inputs_one(rng):
    return heavy(rng, np.ones(R))
def setup_inputs_chain(rng):
    return heavy(rng, np.where(np.arange(R) == 0, 1.0, -1.0))
def setup_inputs_apart(rng):
    d, g = plain(rng), signs(rng)
    v = np.zeros((N, 128, P, 4))
    for r in range(N):
        at = rng.permutation(P)
        a, b = at[:K], at[K:2 * K]
        v[r][np.arange(K), a] = 32 * (1 + rng.random((K, 4)))
        v[r][np.arange(K), b] = 32 * (1 + rng.random((K, 4)))
        v[r][64:96, a] = -(1 + 0.125 * rng.random((32, K, 4)))
        v[r][64:96, at[K:]] = 4096
        v[r][96:, at[K:]] = 1 + rng.random((32, P - K, 4))
    d["c"] = bf(v * g * 2.0 ** 18, N, 128, 4 * P)
    q = (1 + rng.random((N, 128, R, 4))) * g
    q[:, :64] = 0
    d["u"][:, :, :4 * R] = bf(q, N, 128, 4 * R)
    return d
def setup_inputs_ties(rng):
    d, g = plain(rng), signs(rng)
    v = np.abs(d["c"].astype(np.float32)).reshape(N, 128, P, 4)[:, :, :8] * g
    v[:, :, 0] = 0
    h = [rng.permutation(np.arange(P) % 8) for r in range(N)]
    for r in range(0, N, 2):
        i = int(np.flatnonzero(h[r] == 0)[0])
        h[r][i] = h[r][0]
        h[r][0] = 0
    d["c"] = bf(np.stack([v[r][:, h[r]] for r in range(N)]), N, 128, 4 * P)
    d["u"][:, :, :4] = bf(np.abs(d["u"][:, :, :4].astype(np.float32)).reshape(N, 128, 1, 4) * g, N, 128, 4)
    return d
def setup_inputs_spread(rng):
    d = plain(rng)
    d["u"][:, :, 4:8] = 0
    return {**d, "c": big(wide(rng, N, 128, 4 * P, cols=6))}
def check_inputs(d):
    b = []
    for k, low in (("c", 2.0 ** -16), ("u", 2.0 ** -30), ("w", 2.0 ** -30)):
        v = np.abs(d[k].astype(np.float32))
        if not (np.isfinite(v).all() and ((v == 0) | (v >= low) & (v <= 2.0 ** 30)).all()): b.append("a value of " + k)
    if (d["u"][:, :, 4 * R:].astype(np.float32) != 0).any(): b.append("u has numbers behind its first R columns")
    return b
def reference(c, u, w):
    tg = np.zeros((N, R, K), np.float32)
    cs = [mx_ref.quantize(np.ascontiguousarray(c[r])) for r in range(N)]
    qu = [mx_ref.quantize(np.ascontiguousarray(u[r])) for r in range(N)]
    half, zero = np.float32(0.5), np.float32(0)
    for t in range(R):
        left, sent = [], []
        for r in range(N):
            s = mx_ref.matmul(qu[r], cs[r])[t] + zero
            left.append(np.argsort(s, kind="stable")[:K])
            sent.append(pick(cs[r], left[r]))
        for r in range(N):
            a = sent[r ^ (1 << t)]
            z = mx_ref.matmul(pick(a, np.concatenate([np.arange(K), np.full(128 - K, -1)])), cs[r])[:K] + zero
            z[:, left[r]] = -np.inf
            to = np.argmax(z, axis=1)
            merge = np.sort(np.unique(to, return_index=True)[1])
            fill = np.setdiff1d(np.arange(K), merge)
            places = np.sort(left[r])[:len(fill)]
            v = decode(join(cs[r], a)).reshape(128, P + K, 4)
            v[:, to[merge]] = half * v[:, to[merge]] + half * v[:, P + merge]
            new = mx_ref.quantize(np.ascontiguousarray(v[:, :P]).reshape(128, -1).astype(BF))
            q = put(cs[r], to[merge], pick(new, to[merge]))
            cs[r] = put(q, places, pick(a, fill))
            tg[r, t, merge] = to[merge]
            tg[r, t, fill] = -1 - places
    oc, osc, y = np.zeros((N, 128, 4 * P), np.uint8), np.zeros((N, 16, P), np.uint8), np.zeros((N, 128, O * P), np.float32)
    for r in range(N):
        oc[r], osc[r] = emit(cs[r])
        for o in range(O):
            y[r, :, o * P:o * P + P] = mx_ref.matmul(mx_ref.quantize(np.ascontiguousarray(cut(w[r], o))), cs[r])
    return {"oc": oc, "osc": osc, "tg": tg, "y": y}

@@ -1,0 +1,453 @@
+from concourse.mybir import dt, AluOpType, AxisListType, ActivationFunctionType
+
+OP = AluOpType
+AF = ActivationFunctionType
+P, K, R = 256, 48, 3
+WY, WX, WT, WN = 48, 96, 128, 256
+BX, BM, BN = 256, 304, 432
+TINY = 2.0 ** -100
+FAR = 2.0 ** 75
+
+SCRATCH = {}
+for _n, _w in (("cb", 1024), ("us", 16), ("wb", 512), ("up0", 1024), ("up1", 1024), ("up2", 1024), ("cb1", 1024),
+               ("wf", 512), ("on", 520), ("cb2", 1024), ("eb", 520), ("zt", 832), ("r2", 96), ("qrow", 128),
+               ("q16", 128), ("q16m", 128), ("kr", 16), ("kr2", 16), ("rd", 128), ("dm", 80), ("ut", 48), ("h", 512),
+               ("h2", 1024), ("b0", 128), ("b1", 128), ("b2", 48), ("zb1", 704), ("zb2", 784), ("sg", 512)):
+    SCRATCH[_n] = ("sbuf", [128, _w], "bfloat16")
+for _n, _w in (("tri", 128), ("k16", 16), ("jj", 16), ("pc", 32), ("s0", 128), ("s1", 128), ("s2", 256), ("s3", 16),
+               ("s4", 24), ("s5", 256), ("s6", 256), ("x0", 256), ("x1", 256), ("x2", 256), ("y0", 96), ("y1", 96),
+               ("e0", 128), ("e1", 128), ("tr", 96), ("cum0", 256), ("cum1", 256), ("cum2", 256), ("rm", 272), ("dmn", 80),
+               ("dh", 80), ("go", 16), ("yo", 256), ("col", 64), ("tgc", 16)):
+    SCRATCH[_n] = ("sbuf", [128, _w], "float32")
+SCRATCH["pi"] = ("sbuf", [128, 8], "int32")
+SCRATCH["off"] = ("sbuf", [128, 96], "uint16")
+_codes = [("qu0", 256), ("qu1", 256), ("qu2", 256), ("qc1", 512), ("qc2", 256), ("qc3", 512), ("qh", 128), ("qh2", 256),
+          ("qd", 128), ("qct", 128), ("qsg", 128), ("qmg", 128), ("qw", 128), ("ca3", 256)]
+for _t in range(R):
+    _codes += [("ca%d" % _t, P), ("w%d" % _t, WN), ("b%d_" % _t, BN), ("sl%d" % _t, K)]
+for _n, _w in _codes:
+    SCRATCH[_n] = ("sbuf", [128, _w], "float8_e4m3fn_x4")
+    SCRATCH[_n + "s"] = ("sbuf", [128, _w], "uint8")
+for _i in range(8):
+    SCRATCH["p%d" % _i] = ("psum", [128, 512], "float32")
+
+SEMAPHORES = ["sv", "sa", "st", "sg", "ldc0", "ldc1", "ldu", "ldw", "snd", "arr0", "arr1", "arr2", "cp0", "cp1", "cp2",
+              "tg0", "tg1", "tg2", "outs", "osc"]
+
+
+def scheduler(g, T):
+    queue = {"v": g.vector, "a": g.scalar, "t": g.tensor, "g": g, "s": g.sync}
+    count = {"v": 0, "a": 0, "t": 0, "g": 0}
+    seen = {k: {} for k in "vatgs"}
+    clock = {}
+    wr, rd, total = {}, {}, {}
+
+    def need(e, ds):
+        best = {}
+        for s, v in ds:
+            if seen[e].get(s, 0) < v:
+                best[s] = max(best.get(s, 0), v)
+        for s in list(best):
+            for s2 in best:
+                if s2 != s and clock.get((s2, best[s2]), {}).get(s, 0) >= best[s]:
+                    del best[s]
+                    break
+        for s, v in best.items():
+            queue[e].wait_ge(T.sem[s], v)
+            for k2, v2 in clock.get((s, v), {}).items():
+                seen[e][k2] = max(seen[e].get(k2, 0), v2)
+            seen[e][s] = max(seen[e].get(s, 0), v)
+
+    def hit(a, b):
+        if a[1] >= b[2] or b[1] >= a[2]:
+            return False
+        return not (a[3] == b[3] and a[3] > 1 and (a[1] - b[1]) % a[3])
+
+    def deps(reads, writes):
+        d = [ev for r in reads for (q, ev) in wr.get(r[0], []) if hit(r, q)]
+        return d + [ev for w in writes for (q, ev) in wr.get(w[0], []) + rd.get(w[0], []) if hit(w, q)]
+
+    def note(reads, writes, ev):
+        for r in reads:
+            rd.setdefault(r[0], []).append((r, ev))
+        for w in writes:
+            def old(q):
+                return q[1] >= w[1] and q[2] <= w[2] and (w[3] == 1 or (w[3] == q[3] and (q[1] - w[1]) % w[3] == 0))
+            wr[w[0]] = [x for x in wr.get(w[0], []) if not old(x[0])] + [(w, ev)]
+            rd[w[0]] = [x for x in rd.get(w[0], []) if not old(x[0])]
+
+    def op(e, fn, reads, writes):
+        need(e, deps(reads, writes))
+        count[e] += 1
+        ev = ("s" + e, count[e])
+        fn(queue[e]).then_inc(T.sem[ev[0]], 1)
+        clock[ev] = dict(seen[e])
+        note(reads, writes, ev)
+
+    def dma(e, pairs, sem, reads, writes):
+        need(e, deps(reads, writes))
+        for out, in_ in pairs:
+            queue[e].dma_start(out, in_).then_inc(T.sem[sem], 16)
+            total[sem] = total.get(sem, 0) + 16
+        ev = (sem, total[sem])
+        clock[ev] = dict(seen[e])
+        note(reads, writes, ev)
+
+    return op, dma, need, deps, note, count, total
+
+
+def rank_program(g, core, T, topo):
+    rank = T.rank_of(core)
+    if rank is None:
+        return
+    op, dma, need, deps, note, count, total = scheduler(g, T)
+
+    def V(x):
+        return T[x[0]][:, x[1]:x[2]:x[3]] if len(x) == 4 else T[x[0]][:, x[1]:x[2]]
+
+    def opnd(x):
+        return V(x) if isinstance(x, tuple) else x
+
+    def regs(*xs):
+        out = []
+        for x in xs:
+            if isinstance(x, tuple):
+                if x[0][0] == "p" and x[0][1:].isdigit():
+                    out.append((x[0], 0, 512, 1))
+                else:
+                    out.append((x[0], x[1], x[2], x[3] if len(x) == 4 else 1))
+        return out
+
+    def memset(x, c):
+        op("v", lambda q: q.memset(V(x), c), [], regs(x))
+
+    def ts(out, in0, s1, s2, op0, op1=None):
+        if op1 is None:
+            op("v", lambda q: q.tensor_scalar(V(out), V(in0), opnd(s1), None, op0), regs(in0, s1), regs(out))
+        else:
+            op("v", lambda q: q.tensor_scalar(V(out), V(in0), opnd(s1), opnd(s2), op0, op1), regs(in0, s1, s2), regs(out))
+
+    def tt(out, a, b, o):
+        op("v", lambda q: q.tensor_tensor(V(out), V(a), V(b), o), regs(a, b), regs(out))
+
+    def vcopy(out, a):
+        op("v", lambda q: q.tensor_copy(V(out), V(a)), regs(a), regs(out))
+
+    def red(out, a, o, absv=False):
+        kw = {"apply_absolute_value": True} if absv else {}
+        op("v", lambda q: q.tensor_reduce(V(out), V(a), AxisListType.X, o, **kw), regs(a), regs(out))
+
+    def scan(out, a, b, init, op0, op1):
+        op("v", lambda q: q.tensor_tensor_scan(V(out), V(a), V(b), init, op0, op1), regs(a, b), regs(out))
+
+    def act(out, a, fn, bias=None, scale=None, acc=None):
+        kw = {}
+        if bias is not None:
+            kw["bias"] = opnd(bias)
+        if scale is not None:
+            kw["scale"] = opnd(scale)
+        if acc is not None:
+            kw["accum_out"] = V(acc)
+        op("a", lambda q: q.activation(V(out), V(a), fn, **kw), regs(a, bias, scale), regs(out, acc))
+
+    def quant(qn, a, b, src, f, e):
+        op("v", lambda q: q.quantize_mx(T[qn][:, a:b], T[qn + "s"][:, a:b], T[src][:, f:e]),
+           regs((src, f, e)), regs((qn, a, b), (qn + "s", a, b)))
+
+    def mm(pn, l, r, start=True, stop=True):
+        n = r[2] - r[1]
+        reads = regs(l, r, (l[0] + "s", l[1], l[2]), (r[0] + "s", r[1], r[2]))
+        op("t", lambda q: q.matmul_mx(T[pn][:, 0:n], T[l[0]][:, l[1]:l[2]], T[l[0] + "s"][:, l[1]:l[2]],
+                                      T[r[0]][:, r[1]:r[2]], T[r[0] + "s"][:, r[1]:r[2]], start, stop),
+           reads, regs((pn, 0, 512)) if start else [])
+        if not start:
+            note([], regs((pn, 0, 512)), ("st", count["t"]))
+
+    def pick(dst, a, b, src, n, o0, o1):
+        off = ("off", o0, o1)
+        op("v", lambda q: q.tensor_copy(T[dst][:, a:b].bitcast(dt.uint32), T[src][:, 0:n].bitcast(dt.uint32).indirect(V(off))),
+           regs((src, 0, n), off), regs((dst, a, b)))
+        op("a", lambda q: q.activation(T[dst + "s"][:, a:b], T[src + "s"][:, 0:n].indirect(V(off)), AF.Copy),
+           regs((src + "s", 0, n), off), regs((dst + "s", a, b)))
+
+    def iota(out, pattern, base, cm, small=True):
+        kw = {"allow_small_or_imprecise_dtypes": True} if small else {}
+        op("g", lambda q: q.iota(V(out), pattern, base, cm, **kw), [], regs(out))
+
+    def c1(i):
+        return ("col", i, i + 1)
+
+    def pc(i):
+        return ("pc", i, i + 1)
+
+    PF, P16, PH, G16, LT48, D0, D1, D2, NA, NB, AC = 0, 1, 2, 3, 4, 5, 6, 7, 8, 10, 14
+    ASUM, NH, LS, HS, T8, LO_F, HI, H16, CB, SS = 0, 2, 4, 5, 6, 7, 8, 9, 10, 11
+    POSN, EEN, FL, PP, H1, FLP = 12, 16, 20, 21, 22, 23
+    LSUM, SX, KX = 28, 32, 36
+    WLH, WLL, W1, WF = [("qc1", 128 * i, 128 * i + 128) for i in range(4)]
+    WO, WE = [("qc2", 128 * i, 128 * i + 128) for i in range(2)]
+    EB = [("qc3", 128 * i, 128 * i + 128) for i in range(4)]
+
+    dma("a", [(T.us[:, 0:12], T.u[:, 0:12])], "ldu", [], regs(("us", 0, 12)))
+    dma("s", [(T.cb[:, 0:512], T.c[:, 0:512])], "ldc0", [], regs(("cb", 0, 512)))
+    dma("s", [(T.cb[:, 512:1024], T.c[:, 512:1024])], "ldc1", [], regs(("cb", 512, 1024)))
+    dma("s", [(T.wb[:, :], T.w[:, :])], "ldw", [], regs(("wb", 0, 512)))
+
+    iota(("pi", 0, 1), [[1, 1]], 0, 1, False)
+    iota(("qrow", 0, 128), [[1, 128]], 0, 0)
+    iota(("q16", 0, 128), [[0, 8], [1, 16]], 0, 0)
+    iota(("r2", 0, 96), [[32, 3], [0, 2], [2, 16]], -128, 0)
+    iota(("q16m", 0, 128), [[0, 8], [1, 16]], -16, 0)
+    iota(("k16", 0, 16), [[16, 16]], 0, 0)
+    iota(("kr", 0, 16), [[1, 16]], 1, 0)
+    iota(("kr2", 0, 16), [[-2, 16]], 16, 0)
+
+    memset(("zt", 0, 512), 0.0)
+    memset(("on", 0, 520), 1.0)
+    ts(("pi", 1, 2), ("pi", 0, 1), 15, None, OP.bitwise_and)
+    ts(("pi", 2, 3), ("pi", 0, 1), 112, None, OP.bitwise_and)
+    act(("wf", 0, 512), ("on", 0, 512), AF.Copy, scale=-FAR)
+    vcopy(("pc", 0, 3), ("pi", 0, 3))
+    memset(("rm", 256, 272), -2.0 * FAR)
+    memset(("zt", 512, 832), 0.0)
+    act(("cb1", 512, 1024), ("zt", 0, 512), AF.Identity, bias=pc(P16))
+    ts(("cb1", 0, 512), ("zt", 0, 512), pc(PH), None, OP.add)
+    ts(("tri", 0, 128), ("qrow", 0, 128), pc(PF), -TINY, OP.is_lt, OP.mult)
+    act(("h", 0, 512), ("zt", 0, 512), AF.Copy)
+    ts(("cb1", 1, 512, 4), ("on", 0, 128), pc(PH), 128.0, OP.mult, OP.add)
+    for b in range(4):
+        ts(("cb2", 512 + b, 1024, 4), ("qrow", 0, 128), pc(PF), -1.0, OP.is_gt, OP.mult)
+    op("g", lambda q: q.affine_select(V(("eb", 0, 520)), V(("on", 0, 520)), [[-1, 520]], OP.is_equal, 0.0, 4, 4),
+       regs(("on", 0, 520)), regs(("eb", 0, 520)))
+    quant("qc1", 256, 384, "on", 0, 512)
+
+    act(("up0", 3, 512, 4), ("zt", 0, 128), AF.Identity, bias=("us", 3, 4))
+    for b in range(3):
+        ts(("up0", b, 512, 4), ("on", 0, 128), ("us", b, b + 1), None, OP.mult)
+    for b in range(4):
+        ts(("up0", 512 + b, 1024, 4), ("on", 0, 128), ("us", b, b + 1), -1.0, OP.mult, OP.mult)
+    for i in range(2):
+        act(("h2", 512 * i, 512 * i + 512), ("zt", 0, 512), AF.Copy)
+    quant("qu0", 0, 128, "up0", 0, 512)
+    quant("ca0", 0, 128, "cb", 0, 512)
+    quant("qu0", 128, 256, "up0", 512, 1024)
+    quant("ca0", 128, 256, "cb", 512, 1024)
+    quant("qc1", 0, 256, "cb1", 0, 1024)
+
+    def u_tile(t):
+        for b in range(4):
+            act(("up%d" % t, b, 512, 4), ("zt", 0, 128), AF.Identity, bias=("us", 4 * t + b, 4 * t + b + 1))
+        act(("up%d" % t, 512, 1024), ("up%d" % t, 0, 512), AF.Copy, scale=-1.0)
+
+    snd = [0]
+
+    def tg_count(t):
+        ts(c1(CB), ("p0", 0, 1), -1.0, 0.5, OP.mult, OP.add)
+        act(("s6", 0, 256), ("cum%d" % t, 0, 256), AF.Sign, bias=c1(CB), acc=c1(SS))
+
+    def tg_flags(t):
+        ts(c1(FL), c1(EEN + t), 0.5, None, OP.is_gt)
+        ts(c1(PP), c1(POSN + t), 129.0, c1(FL), OP.add, OP.mult)
+        ts(c1(H1), c1(FL), -0.5, 0.5, OP.mult, OP.add)
+        ts(c1(FLP), c1(PP), -129.0, None, OP.add)
+
+    def tg_out(t):
+        ts(("tgc", t, t + 1), c1(SS), c1(H1), c1(FLP), OP.mult, OP.add)
+        dma("s", [(T.tg[t:t + 1, :], T.tgc[0:48, t:t + 1])], "tg%d" % t, regs(("tgc", t, t + 1)), [])
+
+    for t in range(R):
+        ca, W, B, sl = "ca%d" % t, "w%d" % t, "b%d_" % t, "sl%d" % t
+        C0, C1 = (ca, 0, 128), (ca, 128, 256)
+        UP, UN = ("qu%d" % t, 0, 128), ("qu%d" % t, 128, 256)
+        cum = "cum%d" % t
+        o = 32 * t
+        POS, EE = POSN + t, EEN + t
+        MG = 720
+
+        def mg(b):
+            return ("zb2", MG + b, MG + 64, 4)
+
+        mm("p0", C0, UP, True, False)
+        mm("p0", UN, C0, False, True)
+        mm("p2", C0, UP, True, False)
+        mm("p3", UN, C0, True, False)
+        mm("p1", C1, UP, True, False)
+        mm("p1", UN, C1, False, True)
+        mm("p3", C1, UP, False, True)
+        mm("p2", UN, C1, False, True)
+        dma("s", [(T[B][:, 0:P].bitcast(dt.uint8), T[ca][:, 0:P].bitcast(dt.uint8)), (T[B + "s"][:, 0:P], T[ca + "s"][:, 0:P])],
+            "cp%d" % t, regs((ca, 0, P), (ca + "s", 0, P)), regs((B, 0, P), (B + "s", 0, P)))
+        tt(("b0", 0, 128), ("p0", 0, 128), ("tri", 0, 128), OP.is_gt)
+        if t == 0:
+            ts(pc(G16), pc(PF), 16.0, 32.0, OP.is_ge, OP.mult)
+            ts(pc(LT48), pc(PF), 48.0, None, OP.is_lt)
+        scan(("e0", 0, 128), ("b0", 0, 128), ("b0", 0, 128), 0.0, OP.add, OP.add)
+        if t == 0:
+            for c in range(3):
+                ts(pc(NB + c), pc(P16), -1.0, -16.0 * c - 0.5, OP.mult, OP.add)
+        tt(("b1", 0, 128), ("p1", 0, 128), ("tri", 0, 128), OP.is_gt)
+        act(("s1", 0, 128), ("p3", 0, 128), AF.Sign, bias=TINY, acc=c1(ASUM + 1))
+        act(("s0", 0, 128), ("p2", 0, 128), AF.Sign, bias=-TINY, acc=c1(ASUM))
+        if t == 0:
+            ts(("rd", 0, 128), ("qrow", 0, 128), pc(PF), 512.0, OP.not_equal, OP.mult)
+        scan(("e1", 0, 128), ("b1", 0, 128), ("b1", 0, 128), 0.0, OP.add, OP.add)
+        for b in (1, 0):
+            ts(("h", b, 384, 4), ("r2", 0, 96), c1(ASUM + b), ("e%d" % b, 127, 128), OP.subtract, OP.is_equal)
+        quant("qh", 0, 128, "h", 0, 512)
+        act(("col", NH, NH + 2), ("col", ASUM, ASUM + 2), AF.Copy, scale=-1.0, bias=-32.0)
+        mm("p0", WLH, ("qh", 0, 128), True, False)
+        mm("p0", WLL, ("qh", 0, 128), False, True)
+        if t == 0:
+            for b in range(4):
+                ts(("cb2", b, 512, 4), ("q16", 0, 128), pc(P16), None, OP.is_equal)
+            memset(("dm", 0, 80), 0.0)
+        else:
+            quant(W, WY, WN, "zt", 0, 832)
+        op("v", lambda q: q.transpose(T.tr[:, 0:96], T.p0[:, 0:96]), regs(("p0", 0, 96)), regs(("tr", 0, 96)))
+        if t == 0:
+            ts(pc(D1), pc(PF), pc(G16), pc(LT48), OP.subtract, OP.mult)
+        vcopy(("off", o, o + 3), ("tr", 0, 96, 32))
+        if t == 0:
+            ts(pc(D0), pc(G16), float(BM + 80), pc(LT48), OP.add, OP.mult)
+        pick(sl, 0, K, ca, P, o, o + 3)
+        dst = T.cores[rank ^ (1 << t)]
+        rid, pid = topo.addr(dst)[:2]
+        eng = topo.engines(core, dst)[:8]
+        part = (eng[0::2], eng[1::2]) if t == 0 else (eng, eng)
+        mask = [sum(1 << e for e in p) for p in part]
+        n = len(part[0]) + len(part[1])
+        arr = "arr%d" % t
+        need("g", deps(regs((sl, 0, K)), []))
+        g.remote_dma(T[W][:, 0:K].bitcast(dt.uint8), T[sl][:, 0:K].bitcast(dt.uint8), T.sem[arr], T.sem.snd, pid, rid, mask[0])
+        need("g", deps(regs((sl + "s", 0, K)), []))
+        g.remote_dma(T[W + "s"][:, 0:K], T[sl + "s"][:, 0:K], T.sem[arr], T.sem.snd, pid, rid, mask[1])
+        snd[0] += n
+        note([], regs((W, 0, K), (W + "s", 0, K)), (arr, n))
+        if t == 0:
+            iota(("zb2", 0, 720), [[0, 720]], 0, 0)
+            iota(("zb1", 0, 512), [[0, 512]], 0, 0)
+            quant("qc1", 384, 512, "wf", 0, 512)
+        for b in range(2):
+            ts(("h2", 512 * b + b, 512 * b + 512, 4), ("rd", 0, 128), ("e%d" % b, 127, 128), c1(NH + b), OP.add, OP.is_lt)
+        if t == 0:
+            ts(("dm", 0, 48), ("qrow", 0, 48), pc(PF), 16.0, OP.is_equal, OP.mult)
+            ts(("dm", 64, 67), ("k16", 0, 3), pc(PH), 16.0, OP.is_equal, OP.mult)
+        quant("qh2", 0, 256, "h2", 0, 1024)
+        mm("p1", W1, ("qh2", 0, 256))
+        mm("p2", WF, ("qh2", 0, 256), True, False)
+        if t == 0:
+            ts(pc(NA), pc(PF), -1.0, -0.5, OP.mult, OP.add)
+            ts(pc(D2), pc(G16), float(BX), pc(LT48), OP.add, OP.mult)
+            ts(("dmn", 0, 80), ("dm", 0, 80), 61.5, -1000.0, OP.mult, OP.add)
+            quant("qc2", 0, 256, "cb2", 0, 1024)
+        else:
+            mm("p0", ("qct", 0, 128), W1)
+            tg_flags(t - 1)
+        scan((cum, 0, 256), ("p1", 0, 256), ("zt", 0, 256), 0.0, OP.add, OP.add)
+        if t == 0:
+            u_tile(1)
+        act(("s3", 0, 16), (cum, 15, 256, 16), AF.Sign, bias=pc(NA), acc=c1(HS))
+        act(("s2", 0, 256), (cum, 0, 256), AF.Sign, bias=pc(NA), acc=c1(LS))
+        if t == 0:
+            for b in range(4):
+                quant("qc3", 128 * b, 128 * b + 128, "eb", 4 - b, 516 - b)
+            quant(W, WY, WN, "zt", 0, 832)
+        else:
+            tg_count(t - 1)
+        ts(c1(T8), c1(HS), 8.0, None, OP.mult)
+        for b in range(2, 4):
+            ts(mg(b), ("kr2", 0, 16), c1(HS), None, OP.is_equal)
+        ts(c1(LO_F), c1(LS), -0.5, c1(T8), OP.mult, OP.add)
+        if t == 2:
+            quant("qw", 0, 128, "wb", 0, 512)
+        ts(("sg", 2, 512, 4), ("q16", 0, 128), c1(LO_F), pc(D2), OP.is_equal, OP.mult)
+        ts(("sg", 3, 512, 4), ("q16", 0, 128), c1(LO_F), pc(D1), OP.is_equal, OP.mult)
+        if t == 1:
+            u_tile(2)
+        AS, TS = (W, 0, 128), (W, WT, WT + 128)
+        mm("p2", AS, (ca, 0, P), False, True)
+        for b in range(4):
+            mm("p%d" % (4 + b), EB[b], AS, True, False)
+        scan(("rm", 0, 256), ("p2", 0, 256), ("zt", 0, 256), -2.0 * FAR, OP.max, OP.add)
+        act(("s5", 0, 256), ("rm", 0, 256), AF.Sign, scale=-1.0, bias=("rm", 255, 256), acc=c1(POS))
+        ts(("s4", 0, 17), ("rm", 15, 272, 16), ("rm", 255, 256), None, OP.is_lt)
+        if t == 0:
+            ts(("ut", 0, 48), ("qrow", 0, 48), pc(PF), 0.5, OP.is_ge, OP.mult)
+            ts(("jj", 0, 16), ("k16", 0, 16), pc(P16), None, OP.add)
+        red(c1(HI), ("s4", 0, 17), OP.add)
+        if t == 0:
+            ts(("zb2", 258, 268, 4), ("dm", 64, 67), -1.0, None, OP.mult)
+        else:
+            tg_out(t - 1)
+        ts(("dh", 0, 68), ("dmn", 0, 68), c1(HI), 16.0, OP.mult, OP.add)
+        ts(("zb2", 0, 272, 4), ("dm", 0, 68), c1(HI), None, OP.mult)
+        ts(("zb2", 1, 272, 4), ("dh", 0, 68), c1(POS), 0.0, OP.add, OP.max)
+        ts(c1(H16), c1(HI), -16.0, c1(POS), OP.mult, OP.add)
+        quant("qd", 0, 128, "zb2", 0, 512)
+        mm("p1", WO, ("qd", 0, 128))
+        mm("p0", WE, ("qd", 0, 128), True, False)
+        mm("p0", ("qd", 0, 128), W1, False, True)
+        for c in range(3):
+            act(("x%d" % c, 0, 256), (cum, 0, 256), AF.Sign, bias=pc(NB + c), acc=c1(LSUM + c))
+        ts(("sg", 0, 512, 4), ("q16m", 0, 128), c1(H16), pc(D0), OP.is_equal, OP.mult)
+        ts(("sg", 1, 512, 4), ("q16m", 0, 128), c1(H16), pc(D1), OP.is_equal, OP.mult)
+        if t == 0:
+            for c in range(3):
+                ts(pc(AC + c), pc(P16), 16.0 * c, None, OP.add)
+        vcopy(("off", o + 4, o + 7), ("p1", 64, 67))
+        quant("qsg", 0, 128, "sg", 0, 512)
+        pick(W, WT, WT + K, ca, P, o + 4, o + 7)
+        for b in range(4):
+            mm("p%d" % (4 + b), EB[b], TS, False, True)
+        red(c1(EE), ("p0", 0, 48), OP.min, True)
+        ts(("zb1", 0, 192, 4), ("ut", 0, 48), c1(EE), None, OP.is_gt)
+        ts(("off", o + 8, o + 11), ("col", LSUM, LSUM + 3), -0.5, 128.0, OP.mult, OP.add)
+        ts(mg(0), ("kr", 0, 16), c1(HI), c1(EE), OP.is_equal, OP.min)
+        quant("qct", 0, 128, "zb1", 0, 512)
+        ts(mg(1), ("kr", 0, 16), c1(HI), c1(EE), OP.is_equal, OP.min)
+        pick(W, WY, WY + K, ca, P, o + 8, o + 11)
+        quant("qmg", 0, 128, "zb2", 272, 784)
+        mm("p3", W1, ("qct", 0, 128))
+        mm("p1", W1, ("qct", 0, 128))
+        mm("p2", ("qsg", 0, 128), ("qmg", 0, 128))
+        for b in range(2):
+            act(("zb1", 512 + b, 704, 4), ("p%d" % (4 + b), 0, 48), AF.Copy, scale=0.5)
+        for b in range(2, 4):
+            ts(("zb1", 512 + b, 704, 4), ("p%d" % (4 + b), 0, 48), 0.5, None, OP.mult)
+        for c in range(2):
+            act(("y%d" % c, 0, 96), ("p3", 0, 96), AF.Sign, bias=pc(NB + c), acc=c1(SX + c))
+        ts(("b2", 0, 48), ("p1", 0, 48), pc(AC + 2), None, OP.is_le)
+        for c in range(3):
+            ts(c1(KX + c), ("p1", 47, 48), pc(AC + c), pc(AC + c), OP.is_le, OP.mult)
+        red(c1(SX + 2), ("b2", 0, 48), OP.add)
+        tt(("go", 0, 16), ("p2", 112, 128), ("jj", 0, 16), OP.max)
+        for c in range(2):
+            ts(("off", o + 12 + c, o + 13 + c), c1(SX + c), -0.5, c1(KX + c), OP.mult, OP.add)
+        vcopy(("off", o + 16, o + 32), ("go", 0, 16))
+        ts(("off", o + 14, o + 15), c1(SX + 2), c1(KX + 2), None, OP.add)
+        if t == R - 1:
+            mm("p0", ("qct", 0, 128), W1)
+        quant(B, BM, BN, "zb1", 192, 704)
+        pick(B, BX, BX + K, W, WX, o + 12, o + 15)
+        nx = "ca%d" % (t + 1)
+        if t < R - 1:
+            quant("qu%d" % (t + 1), 0, 128, "up%d" % (t + 1), 0, 512)
+        else:
+            tg_count(t)
+        pick(nx, 0, 128, B, BN, o + 16, o + 24)
+        if t < R - 1:
+            quant("qu%d" % (t + 1), 128, 256, "up%d" % (t + 1), 512, 1024)
+        pick(nx, 128, 256, B, BN, o + 24, o + 32)
+
+    for i in range(2):
+        a, b = 128 * i, 128 * i + 128
+        dma("s", [(T.oc[:, 4 * a:4 * b], T.ca3[:, a:b].bitcast(dt.uint8))], "outs", regs(("ca3", a, b)), [])
+        mm("p%d" % (1 + 2 * i), ("qw", 0, 128), ("ca3", a, b))
+    dma("a", [(T.osc[4 * k:4 * k + 4, 0:P], T.ca3s[32 * k:32 * k + 4, 0:P]) for k in range(4)], "osc", regs(("ca3s", 0, P)), [])
+    tg_flags(R - 1)
+    vcopy(("yo", 0, 128), ("p1", 0, 128))
+    tg_out(R - 1)
+    vcopy(("yo", 128, 256), ("p3", 0, 128))
+    dma("s", [(T.y[:, :], T.yo[:, :])], "outs", regs(("yo", 0, 256)), [])
+    g.wait_ge(T.sem.snd, snd[0])
+    need("s", [("s" + e, count[e]) for e in "vatg"] + [(s, v) for s, v in total.items()])

@@ -34,6 +34,25 @@ for _i in range(8):
 SEMAPHORES = ["sv", "sa", "st", "sg", "ldc0", "ldc1", "ldu", "ldw", "snd", "arr0", "arr1", "arr2", "cp0", "cp1", "cp2",
               "tg0", "tg1", "tg2", "outs", "osc"]
 
+ORDER = [1,77,13,4,14,15,12,0,34,31,32,33,17,19,21,24,35,37,38,36,42,41,43,46,47,49,2,44,54,50,3,5,22,6,7,8,29,10,11,9,
+         86,20,45,55,23,51,62,48,56,58,52,66,102,63,67,53,64,68,61,57,69,81,27,30,40,128,101,16,70,96,39,65,25,71,72,78,
+         75,80,18,82,90,83,84,85,103,92,89,97,127,73,93,146,74,79,130,104,26,109,91,241,94,100,59,144,98,106,112,76,28,
+         88,95,242,113,108,111,114,107,139,116,117,99,145,60,140,119,124,125,126,129,115,186,131,133,118,132,135,120,110,
+         244,141,134,142,157,143,123,136,147,150,149,137,138,121,155,105,154,122,152,151,153,167,170,243,169,168,148,87,
+         156,160,158,159,165,163,161,164,171,173,174,175,176,177,166,178,182,172,180,179,183,181,184,189,187,190,162,185,
+         188,192,193,201,191,200,196,197,203,202,206,226,195,245,198,204,207,194,199,205,208,209,210,228,220,227,221,211,
+         212,214,215,217,225,229,216,218,222,223,213,362,230,233,234,231,232,235,238,266,224,219,246,251,236,253,254,237,
+         257,252,258,260,312,259,239,261,269,309,247,248,262,263,264,249,250,265,267,280,255,270,240,278,272,273,276,274,
+         290,275,291,268,279,283,281,282,288,292,285,287,294,277,293,286,271,284,296,297,298,299,300,289,301,305,295,303,
+         302,306,307,304,308,311,310,315,316,313,324,314,256,319,320,326,325,318,321,327,329,330,317,322,328,331,332,334,
+         335,349,333,350,344,343,337,348,338,340,339,341,345,336,346,353,354,358,360,359,355,356,357,385,347,342,365,370,
+         371,361,372,352,373,366,367,363,376,377,384,378,380,381,382,383,369,368,379,387,364,386,399,388,389,351,391,392,
+         394,395,393,397,390,398,400,402,401,407,406,396,405,408,403,409,415,416,417,418,419,420,424,410,411,413,412,414,
+         422,421,423,426,425,429,374,404,427,323,431,428,432,436,433,435,437,434,430,438,440,441,444,447,448,449,375,442,
+         443,439,445,446]
+OTHER = {24,32,33,34,59,60,83,96,98,103,116,128,130,131,132,134,144,169,170,210,233,238,242,255,258,260,292,293,333,351,
+         358,374,379,409,411,412,429,442,443,445}
+
 
 def scheduler(g, T):
     queue = {"v": g.vector, "a": g.scalar, "t": g.tensor, "g": g, "s": g.sync}
@@ -77,7 +96,8 @@ def scheduler(g, T):
             rd[w[0]] = [x for x in rd.get(w[0], []) if not old(x[0])]
 
     def op(e, fn, reads, writes):
-        need(e, deps(reads, writes))
+        bank = [ev for r in reads if r[0][1:].isdigit() and r[0][0] == "p" for (q, ev) in rd.get(r[0], []) if ev[0] != "s" + e]
+        need(e, deps(reads, writes) + bank)
         count[e] += 1
         ev = ("s" + e, count[e])
         fn(queue[e]).then_inc(T.sem[ev[0]], 1)
@@ -100,7 +120,35 @@ def rank_program(g, core, T, topo):
     rank = T.rank_of(core)
     if rank is None:
         return
-    op, dma, need, deps, note, count, total = scheduler(g, T)
+    op0, dma0, need, deps, note, count, total = scheduler(g, T)
+    items = []
+
+    def op(e, fn, reads, writes, alt=None, acc=None):
+        items.append(("op", e, fn, reads, writes, alt, acc))
+
+    def dma(e, pairs, sem, reads, writes):
+        items.append(("dma", e, pairs, reads, writes, None, sem))
+
+    def send(out, in_, mask, reads, writes, ev, pid, rid):
+        def fn():
+            need("g", deps(reads, []))
+            g.remote_dma(out, in_, T.sem[ev[0]], T.sem.snd, pid, rid, mask)
+            note([], writes, ev)
+        items.append(("send", "g", fn, reads, writes, None, ev))
+
+    def issue():
+        for i in (ORDER or range(len(items))):
+            kind, e, fn, reads, writes, alt, x = items[i]
+            if kind == "send":
+                fn()
+            elif kind == "dma":
+                dma0(e, fn, x, reads, writes)
+            else:
+                if i in OTHER:
+                    e, fn = alt
+                op0(e, fn, reads, writes)
+                if x:
+                    note([], x, ("st", count["t"]))
 
     def V(x):
         return T[x[0]][:, x[1]:x[2]:x[3]] if len(x) == 4 else T[x[0]][:, x[1]:x[2]]
@@ -118,10 +166,27 @@ def rank_program(g, core, T, topo):
                     out.append((x[0], x[1], x[2], x[3] if len(x) == 4 else 1))
         return out
 
+    def lin(out, a, scale, bias, e="v"):
+        kw = {k: opnd(x) for k, x in (("scale", scale), ("bias", bias)) if x is not None}
+        fa = AF.Identity if isinstance(scale, tuple) or isinstance(bias, tuple) else AF.Copy
+        args = [(opnd(x), o) for x, o in ((scale, OP.mult), (bias, OP.add)) if x is not None] or [(1.0, OP.mult)]
+
+        def fv(q):
+            if len(args) == 1:
+                return q.tensor_scalar(V(out), V(a), args[0][0], None, args[0][1])
+            return q.tensor_scalar(V(out), V(a), args[0][0], args[1][0], OP.mult, OP.add)
+        both = {"v": fv, "a": lambda q: q.activation(V(out), V(a), fa, **kw)}
+        o = "a" if e == "v" else "v"
+        op(e, both[e], regs(a, scale, bias), regs(out), (o, both[o]))
+
     def memset(x, c):
         op("v", lambda q: q.memset(V(x), c), [], regs(x))
 
     def ts(out, in0, s1, s2, op0, op1=None):
+        if out[0] not in ("off", "pi") and (op0, op1) in ((OP.mult, None), (OP.mult, OP.add)):
+            return lin(out, in0, s1, s2)
+        if out[0] not in ("off", "pi") and (op0, op1) == (OP.add, None):
+            return lin(out, in0, None, s1)
         if op1 is None:
             op("v", lambda q: q.tensor_scalar(V(out), V(in0), opnd(s1), None, op0), regs(in0, s1), regs(out))
         else:
@@ -141,6 +206,8 @@ def rank_program(g, core, T, topo):
         op("v", lambda q: q.tensor_tensor_scan(V(out), V(a), V(b), init, op0, op1), regs(a, b), regs(out))
 
     def act(out, a, fn, bias=None, scale=None, acc=None):
+        if fn in (AF.Copy, AF.Identity):
+            return lin(out, a, scale, bias, "a")
         kw = {}
         if bias is not None:
             kw["bias"] = opnd(bias)
@@ -159,16 +226,15 @@ def rank_program(g, core, T, topo):
         reads = regs(l, r, (l[0] + "s", l[1], l[2]), (r[0] + "s", r[1], r[2]))
         op("t", lambda q: q.matmul_mx(T[pn][:, 0:n], T[l[0]][:, l[1]:l[2]], T[l[0] + "s"][:, l[1]:l[2]],
                                       T[r[0]][:, r[1]:r[2]], T[r[0] + "s"][:, r[1]:r[2]], start, stop),
-           reads, regs((pn, 0, 512)) if start else [])
-        if not start:
-            note([], regs((pn, 0, 512)), ("st", count["t"]))
+           reads, regs((pn, 0, 512)) if start else [], None, None if start else regs((pn, 0, 512)))
 
     def pick(dst, a, b, src, n, o0, o1):
         off = ("off", o0, o1)
         op("v", lambda q: q.tensor_copy(T[dst][:, a:b].bitcast(dt.uint32), T[src][:, 0:n].bitcast(dt.uint32).indirect(V(off))),
            regs((src, 0, n), off), regs((dst, a, b)))
         op("a", lambda q: q.activation(T[dst + "s"][:, a:b], T[src + "s"][:, 0:n].indirect(V(off)), AF.Copy),
-           regs((src + "s", 0, n), off), regs((dst + "s", a, b)))
+           regs((src + "s", 0, n), off), regs((dst + "s", a, b)),
+           ("v", lambda q: q.tensor_copy(T[dst + "s"][:, a:b], T[src + "s"][:, 0:n].indirect(V(off)))))
 
     def iota(out, pattern, base, cm, small=True):
         kw = {"allow_small_or_imprecise_dtypes": True} if small else {}
@@ -223,7 +289,7 @@ def rank_program(g, core, T, topo):
 
     act(("up0", 3, 512, 4), ("zt", 0, 128), AF.Identity, bias=("us", 3, 4))
     for b in range(3):
-        ts(("up0", b, 512, 4), ("on", 0, 128), ("us", b, b + 1), None, OP.mult)
+        lin(("up0", b, 512, 4), ("zt", 0, 128), None, ("us", b, b + 1))
     for b in range(4):
         ts(("up0", 512 + b, 1024, 4), ("on", 0, 128), ("us", b, b + 1), -1.0, OP.mult, OP.mult)
     for i in range(2):
@@ -317,12 +383,11 @@ def rank_program(g, core, T, topo):
         mask = [sum(1 << e for e in p) for p in part]
         n = len(part[0]) + len(part[1])
         arr = "arr%d" % t
-        need("g", deps(regs((sl, 0, K)), []))
-        g.remote_dma(T[W][:, 0:K].bitcast(dt.uint8), T[sl][:, 0:K].bitcast(dt.uint8), T.sem[arr], T.sem.snd, pid, rid, mask[0])
-        need("g", deps(regs((sl + "s", 0, K)), []))
-        g.remote_dma(T[W + "s"][:, 0:K], T[sl + "s"][:, 0:K], T.sem[arr], T.sem.snd, pid, rid, mask[1])
+        send(T[W][:, 0:K].bitcast(dt.uint8), T[sl][:, 0:K].bitcast(dt.uint8), mask[0], regs((sl, 0, K)), regs((W, 0, K)),
+             (arr, n), pid, rid)
+        send(T[W + "s"][:, 0:K], T[sl + "s"][:, 0:K], mask[1], regs((sl + "s", 0, K)), regs((W + "s", 0, K)),
+             (arr, n), pid, rid)
         snd[0] += n
-        note([], regs((W, 0, K), (W + "s", 0, K)), (arr, n))
         if t == 0:
             iota(("zb2", 0, 720), [[0, 720]], 0, 0)
             iota(("zb1", 0, 512), [[0, 512]], 0, 0)
@@ -445,9 +510,11 @@ def rank_program(g, core, T, topo):
         mm("p%d" % (1 + 2 * i), ("qw", 0, 128), ("ca3", a, b))
     dma("a", [(T.osc[4 * k:4 * k + 4, 0:P], T.ca3s[32 * k:32 * k + 4, 0:P]) for k in range(4)], "osc", regs(("ca3s", 0, P)), [])
     tg_flags(R - 1)
-    vcopy(("yo", 0, 128), ("p1", 0, 128))
+    lin(("yo", 0, 128), ("p1", 0, 128), None, None)
     tg_out(R - 1)
-    vcopy(("yo", 128, 256), ("p3", 0, 128))
-    dma("s", [(T.y[:, :], T.yo[:, :])], "outs", regs(("yo", 0, 256)), [])
+    lin(("yo", 128, 256), ("p3", 0, 128), None, None)
+    for a in (0, 128):
+        dma("s", [(T.y[:, a:a + 128], T.yo[:, a:a + 128])], "outs", regs(("yo", a, a + 128)), [])
+    issue()
     g.wait_ge(T.sem.snd, snd[0])
     need("s", [("s" + e, count[e]) for e in "vatg"] + [(s, v) for s, v in total.items()])

@@ -3,28 +3,27 @@ from concourse.mybir import dt, AluOpType, AxisListType, ActivationFunctionType
 OP = AluOpType
 AF = ActivationFunctionType
 P, K, R = 256, 48, 3
-WY, WX, WT, WN = 48, 96, 128, 256
-BX, BM, BN = 256, 304, 432
+BC, BX, BM, BN = 48, 320, 384, 432
 TINY = 2.0 ** -100
 FAR = 2.0 ** 75
+NEG, ON, ZR, EO, TA = 208, 336, 848, 864, 1376
 
 SCRATCH = {}
-for _n, _w in (("cb", 1024), ("us", 16), ("wb", 512), ("up0", 1024), ("up1", 1024), ("up2", 1024), ("cb1", 1024),
-               ("wf", 512), ("on", 520), ("cb2", 1024), ("eb", 520), ("zt", 832), ("r2", 96), ("qrow", 128),
-               ("q16", 128), ("q16m", 128), ("kr", 16), ("kr2", 16), ("rd", 128), ("dm", 80), ("ut", 48), ("h", 512),
-               ("h2", 1024), ("b0", 128), ("b1", 128), ("b2", 48), ("zb1", 704), ("zb2", 784), ("sg", 512)):
+for _n, _w in (("cb", 1024), ("us", 16), ("wb", 512), ("up0", 1024), ("up1", 1024), ("up2", 1024), ("ta", TA), ("tb", 768),
+               ("tc", 708), ("td", 896), ("wf", 512), ("h2", 1088), ("rd", 576), ("r2", 192), ("qrow", 128), ("q16", 128),
+               ("q16m", 128), ("kr", 32), ("dm", 104), ("dmn", 104), ("dh", 104), ("ut", 48), ("b0", 128), ("b1", 128),
+               ("tri", 128), ("sg", 512), ("f0", 128), ("f1", 128), ("s0", 128), ("s1", 128),
+               ("s4", 32), ("s5", 256), ("s6", 256), ("y0", 48), ("y1", 48), ("y2", 48)):
     SCRATCH[_n] = ("sbuf", [128, _w], "bfloat16")
-for _n, _w in (("tri", 128), ("k16", 16), ("jj", 16), ("pc", 32), ("s0", 128), ("s1", 128), ("s2", 256), ("s3", 16),
-               ("s4", 24), ("s5", 256), ("s6", 256), ("x0", 256), ("x1", 256), ("x2", 256), ("y0", 96), ("y1", 96),
-               ("e0", 128), ("e1", 128), ("tr", 96), ("cum0", 256), ("cum1", 256), ("cum2", 256), ("rm", 272), ("dmn", 80),
-               ("dh", 80), ("go", 16), ("yo", 256), ("col", 64), ("tgc", 16)):
+for _n, _w in (("k16", 16), ("jj", 16), ("pc", 16), ("usf", 16), ("tr", 96), ("rm", 272), ("go", 64), ("yo", 256),
+               ("col", 32), ("tgc", 16), ("e0", 128), ("e1", 128)):
     SCRATCH[_n] = ("sbuf", [128, _w], "float32")
 SCRATCH["pi"] = ("sbuf", [128, 8], "int32")
 SCRATCH["off"] = ("sbuf", [128, 96], "uint16")
-_codes = [("qu0", 256), ("qu1", 256), ("qu2", 256), ("qc1", 512), ("qc2", 256), ("qc3", 512), ("qh", 128), ("qh2", 256),
-          ("qd", 128), ("qct", 128), ("qsg", 128), ("qmg", 128), ("qw", 128), ("ca3", 256)]
+_codes = [("qu0", 256), ("qu1", 256), ("qu2", 256), ("qc", 388), ("qwl", 128), ("qwa", 128), ("qwf", 128), ("qe", 512),
+          ("qh", 128), ("qh2", 272), ("qd", 128), ("qz", 128), ("qsg", 128), ("qw", 128), ("ca3", 256)]
 for _t in range(R):
-    _codes += [("ca%d" % _t, P), ("w%d" % _t, WN), ("b%d_" % _t, BN), ("sl%d" % _t, K)]
+    _codes += [("ca%d" % _t, P), ("w%d" % _t, 128), ("b%d_" % _t, 512), ("sl%d" % _t, K)]
 for _n, _w in _codes:
     SCRATCH[_n] = ("sbuf", [128, _w], "float8_e4m3fn_x4")
     SCRATCH[_n + "s"] = ("sbuf", [128, _w], "uint8")
@@ -32,26 +31,10 @@ for _i in range(8):
     SCRATCH["p%d" % _i] = ("psum", [128, 512], "float32")
 
 SEMAPHORES = ["sv", "sa", "st", "sg", "ldc0", "ldc1", "ldu", "ldw", "snd", "arr0", "arr1", "arr2", "cp0", "cp1", "cp2",
-              "tg0", "tg1", "tg2", "outs", "osc"]
+              "cw0", "cw1", "dup", "tg0", "tg1", "tg2", "outs", "osc"]
 
-ORDER = [1,77,13,4,14,15,12,0,34,31,32,33,17,19,21,24,35,37,38,36,42,41,43,46,47,49,2,44,54,50,3,5,22,6,7,8,29,10,11,9,
-         86,20,45,55,23,51,62,48,56,58,52,66,102,63,67,53,64,68,61,57,69,81,27,30,40,128,101,16,70,96,39,65,25,71,72,78,
-         75,80,18,82,90,83,84,85,103,92,89,97,127,73,93,146,74,79,130,104,26,109,91,241,94,100,59,144,98,106,112,76,28,
-         88,95,242,113,108,111,114,107,139,116,117,99,145,60,140,119,124,125,126,129,115,186,131,133,118,132,135,120,110,
-         244,141,134,142,157,143,123,136,147,150,149,137,138,121,155,105,154,122,152,151,153,167,170,243,169,168,148,87,
-         156,160,158,159,165,163,161,164,171,173,174,175,176,177,166,178,182,172,180,179,183,181,184,189,187,190,162,185,
-         188,192,193,201,191,200,196,197,203,202,206,226,195,245,198,204,207,194,199,205,208,209,210,228,220,227,221,211,
-         212,214,215,217,225,229,216,218,222,223,213,362,230,233,234,231,232,235,238,266,224,219,246,251,236,253,254,237,
-         257,252,258,260,312,259,239,261,269,309,247,248,262,263,264,249,250,265,267,280,255,270,240,278,272,273,276,274,
-         290,275,291,268,279,283,281,282,288,292,285,287,294,277,293,286,271,284,296,297,298,299,300,289,301,305,295,303,
-         302,306,307,304,308,311,310,315,316,313,324,314,256,319,320,326,325,318,321,327,329,330,317,322,328,331,332,334,
-         335,349,333,350,344,343,337,348,338,340,339,341,345,336,346,353,354,358,360,359,355,356,357,385,347,342,365,370,
-         371,361,372,352,373,366,367,363,376,377,384,378,380,381,382,383,369,368,379,387,364,386,399,388,389,351,391,392,
-         394,395,393,397,390,398,400,402,401,407,406,396,405,408,403,409,415,416,417,418,419,420,424,410,411,413,412,414,
-         422,421,423,426,425,429,374,404,427,323,431,428,432,436,433,435,437,434,430,438,440,441,444,447,448,449,375,442,
-         443,439,445,446]
-OTHER = {24,32,33,34,59,60,83,96,98,103,116,128,130,131,132,134,144,169,170,210,233,238,242,255,258,260,292,293,333,351,
-         358,374,379,409,411,412,429,442,443,445}
+ORDER = [60,4,0,5,1,12,14,15,29,30,11,16,36,9,22,42,35,40,18,17,34,77,21,73,72,2,75,74,10,79,6,76,78,81,80,3,38,19,95,20,59,32,23,96,8,7,99,100,64,39,93,97,104,106,105,87,94,102,89,98,101,83,109,107,108,13,110,111,31,103,112,122,85,113,37,120,114,51,115,44,116,67,24,82,68,71,41,45,53,90,88,70,46,84,69,52,121,62,47,43,54,117,55,118,119,28,33,26,123,27,124,126,25,57,48,91,61,63,131,50,130,128,58,56,132,125,134,133,65,136,137,135,138,127,142,129,141,139,140,92,144,49,145,143,153,152,146,154,147,148,66,86,156,155,149,168,157,162,170,163,158,169,150,151,159,164,160,171,165,161,172,181,166,167,177,173,174,175,178,184,185,176,193,179,186,188,192,189,191,198,187,195,190,194,197,196,199,200,180,201,210,202,203,182,204,206,205,207,209,211,212,208,213,215,220,221,223,224,222,225,226,227,228,230,231,232,229,233,234,219,242,236,214,217,218,241,235,216,238,243,245,244,239,247,252,240,257,259,258,248,249,251,260,253,237,246,254,256,270,266,267,250,261,255,262,264,263,265,273,274,275,268,282,277,278,284,283,280,287,285,288,276,279,286,289,269,290,300,291,183,292,271,293,294,298,281,296,295,299,301,303,302,297,304,309,310,308,312,313,311,314,315,316,317,318,307,319,320,321,322,305,323,331,330,355,325,306,324,327,336,359,332,334,333,346,348,329,342,347,338,349,326,328,340,356,341,335,343,337,350,272,344,345,339,357,351,352,363,362,353,358,364,354,365,367,360,366,369,361,368,370]
+OTHER = {17,19,20,21,22,55,63,64,135,158,159,180,247,248,249,269,338,358}
 
 
 def scheduler(g, T):
@@ -183,10 +166,6 @@ def rank_program(g, core, T, topo):
         op("v", lambda q: q.memset(V(x), c), [], regs(x))
 
     def ts(out, in0, s1, s2, op0, op1=None):
-        if out[0] not in ("off", "pi") and (op0, op1) in ((OP.mult, None), (OP.mult, OP.add)):
-            return lin(out, in0, s1, s2)
-        if out[0] not in ("off", "pi") and (op0, op1) == (OP.add, None):
-            return lin(out, in0, None, s1)
         if op1 is None:
             op("v", lambda q: q.tensor_scalar(V(out), V(in0), opnd(s1), None, op0), regs(in0, s1), regs(out))
         else:
@@ -206,8 +185,6 @@ def rank_program(g, core, T, topo):
         op("v", lambda q: q.tensor_tensor_scan(V(out), V(a), V(b), init, op0, op1), regs(a, b), regs(out))
 
     def act(out, a, fn, bias=None, scale=None, acc=None):
-        if fn in (AF.Copy, AF.Identity):
-            return lin(out, a, scale, bias, "a")
         kw = {}
         if bias is not None:
             kw["bias"] = opnd(bias)
@@ -217,7 +194,8 @@ def rank_program(g, core, T, topo):
             kw["accum_out"] = V(acc)
         op("a", lambda q: q.activation(V(out), V(a), fn, **kw), regs(a, bias, scale), regs(out, acc))
 
-    def quant(qn, a, b, src, f, e):
+    def quant(qn, a, b, src, f):
+        e = f + 4 * (b - a)
         op("v", lambda q: q.quantize_mx(T[qn][:, a:b], T[qn + "s"][:, a:b], T[src][:, f:e]),
            regs((src, f, e)), regs((qn, a, b), (qn + "s", a, b)))
 
@@ -236,6 +214,15 @@ def rank_program(g, core, T, topo):
            regs((src + "s", 0, n), off), regs((dst + "s", a, b)),
            ("v", lambda q: q.tensor_copy(T[dst + "s"][:, a:b], T[src + "s"][:, 0:n].indirect(V(off)))))
 
+    def copy(sem, *moves):
+        pairs, reads, writes = [], [], []
+        for dst, a, src, f, n in moves:
+            pairs += [(T[dst][:, a:a + n].bitcast(dt.uint8), T[src][:, f:f + n].bitcast(dt.uint8)),
+                      (T[dst + "s"][:, a:a + n], T[src + "s"][:, f:f + n])]
+            reads += regs((src, f, f + n), (src + "s", f, f + n))
+            writes += regs((dst, a, a + n), (dst + "s", a, a + n))
+        dma("s", pairs, sem, reads, writes)
+
     def iota(out, pattern, base, cm, small=True):
         kw = {"allow_small_or_imprecise_dtypes": True} if small else {}
         op("g", lambda q: q.iota(V(out), pattern, base, cm, **kw), [], regs(out))
@@ -246,13 +233,15 @@ def rank_program(g, core, T, topo):
     def pc(i):
         return ("pc", i, i + 1)
 
-    PF, P16, PH, G16, LT48, D0, D1, D2, NA, NB, AC = 0, 1, 2, 3, 4, 5, 6, 7, 8, 10, 14
-    ASUM, NH, LS, HS, T8, LO_F, HI, H16, CB, SS = 0, 2, 4, 5, 6, 7, 8, 9, 10, 11
-    POSN, EEN, FL, PP, H1, FLP = 12, 16, 20, 21, 22, 23
-    LSUM, SX, KX = 28, 32, 36
-    WLH, WLL, W1, WF = [("qc1", 128 * i, 128 * i + 128) for i in range(4)]
-    WO, WE = [("qc2", 128 * i, 128 * i + 128) for i in range(2)]
-    EB = [("qc3", 128 * i, 128 * i + 128) for i in range(4)]
+    def on(n):
+        return ("ta", ON, ON + n)
+
+    PF, P16, PH, PH1, G16, LT48, D0, D1, NB = 0, 1, 2, 3, 4, 5, 6, 7, 8
+    ASUM, HI, H16, POSN, EEN, SX, SS, UU, MF = 0, 2, 3, 4, 8, 12, 16, 20, 24
+    W1, W256, W48, WEO = ("qc", 128, 256), ("qc", 0, 256), ("qc", 208, 336), ("qc", 260, 388)
+    WL, WA, WF = ("qwl", 0, 128), ("qwa", 0, 128), ("qwf", 0, 128)
+    EB = [("qe", 128 * i, 128 * i + 128) for i in range(4)]
+    QH, QD, QZ, QS = ("qh", 0, 128), ("qd", 0, 128), ("qz", 0, 128), ("qsg", 0, 128)
 
     dma("a", [(T.us[:, 0:12], T.u[:, 0:12])], "ldu", [], regs(("us", 0, 12)))
     dma("s", [(T.cb[:, 0:512], T.c[:, 0:512])], "ldc0", [], regs(("cb", 0, 512)))
@@ -261,77 +250,91 @@ def rank_program(g, core, T, topo):
 
     iota(("pi", 0, 1), [[1, 1]], 0, 1, False)
     iota(("qrow", 0, 128), [[1, 128]], 0, 0)
+    for b in range(2):
+        iota(("r2", b, 192, 2), [[32, 3], [0, 2], [2, 16]], -96, 0)
     iota(("q16", 0, 128), [[0, 8], [1, 16]], 0, 0)
-    iota(("r2", 0, 96), [[32, 3], [0, 2], [2, 16]], -128, 0)
-    iota(("q16m", 0, 128), [[0, 8], [1, 16]], -16, 0)
     iota(("k16", 0, 16), [[16, 16]], 0, 0)
-    iota(("kr", 0, 16), [[1, 16]], 1, 0)
-    iota(("kr2", 0, 16), [[-2, 16]], 16, 0)
+    iota(("kr", 0, 32), [[1, 16], [0, 2]], 1, 0)
 
-    memset(("zt", 0, 512), 0.0)
-    memset(("on", 0, 520), 1.0)
+    memset(("ta", NEG, ON), -1.0)
+    memset(on(512), 1.0)
+    memset(("ta", ZR, EO), 0.0)
     ts(("pi", 1, 2), ("pi", 0, 1), 15, None, OP.bitwise_and)
     ts(("pi", 2, 3), ("pi", 0, 1), 112, None, OP.bitwise_and)
-    act(("wf", 0, 512), ("on", 0, 512), AF.Copy, scale=-FAR)
     vcopy(("pc", 0, 3), ("pi", 0, 3))
-    memset(("rm", 256, 272), -2.0 * FAR)
-    memset(("zt", 512, 832), 0.0)
-    act(("cb1", 512, 1024), ("zt", 0, 512), AF.Identity, bias=pc(P16))
-    ts(("cb1", 0, 512), ("zt", 0, 512), pc(PH), None, OP.add)
+    lin(pc(PH1), pc(PH), None, 128.0)
     ts(("tri", 0, 128), ("qrow", 0, 128), pc(PF), -TINY, OP.is_lt, OP.mult)
-    act(("h", 0, 512), ("zt", 0, 512), AF.Copy)
-    ts(("cb1", 1, 512, 4), ("on", 0, 128), pc(PH), 128.0, OP.mult, OP.add)
+    for b, x in enumerate((PH, PH1, P16, P16)):
+        lin(("td", 384 + b, 896, 4), on(128), pc(x), None)
+    quant("qwl", 0, 128, "td", 384)
+    op("g", lambda q: q.affine_select(V(("tc", 192, 708)), V(on(516)), [[-1, 516]], OP.is_equal, 0.0, 3, 4),
+       regs(on(516)), regs(("tc", 192, 708)))
     for b in range(4):
-        ts(("cb2", 512 + b, 1024, 4), ("qrow", 0, 128), pc(PF), -1.0, OP.is_gt, OP.mult)
-    op("g", lambda q: q.affine_select(V(("eb", 0, 520)), V(("on", 0, 520)), [[-1, 520]], OP.is_equal, 0.0, 4, 4),
-       regs(("on", 0, 520)), regs(("eb", 0, 520)))
-    quant("qc1", 256, 384, "on", 0, 512)
-
-    act(("up0", 3, 512, 4), ("zt", 0, 128), AF.Identity, bias=("us", 3, 4))
-    for b in range(3):
-        lin(("up0", b, 512, 4), ("zt", 0, 128), None, ("us", b, b + 1))
+        quant("qe", 128 * b, 128 * b + 128, "tc", 195 - b)
     for b in range(4):
-        ts(("up0", 512 + b, 1024, 4), ("on", 0, 128), ("us", b, b + 1), -1.0, OP.mult, OP.mult)
-    for i in range(2):
-        act(("h2", 512 * i, 512 * i + 512), ("zt", 0, 512), AF.Copy)
-    quant("qu0", 0, 128, "up0", 0, 512)
-    quant("ca0", 0, 128, "cb", 0, 512)
-    quant("qu0", 128, 256, "up0", 512, 1024)
-    quant("ca0", 128, 256, "cb", 512, 1024)
-    quant("qc1", 0, 256, "cb1", 0, 1024)
+        memset(("wf", b, 512, 4), -FAR if b < 2 else 0.0)
+    quant("qwf", 0, 128, "wf", 0)
+    ts(("rd", 0, 256, 2), ("qrow", 0, 128), pc(PF), -512.0, OP.not_equal, OP.mult)
+    ts(("rd", 1, 256, 2), ("qrow", 0, 128), pc(PF), -512.0, OP.is_le, OP.mult)
+    memset(("rd", 288, 544, 2), -512.0)
+    memset(("rd", 289, 544, 2), 0.0)
+    for a, x in ((256, PH1), (544, PH)):
+        ts(("rd", a, a + 32, 2), ("k16", 0, 16), pc(x), -512.0, OP.is_le, OP.mult)
+        ts(("rd", a + 1, a + 32, 2), ("k16", 0, 16), pc(x), -512.0, OP.not_equal, OP.mult)
+    memset(("h2", 1, 512, 2), 0.0)
+    for b in range(2):
+        ts(("ta", EO + b, TA, 4), ("qrow", 0, 128), pc(PF), -1.0, OP.is_gt, OP.mult)
+        ts(("ta", EO + 2 + b, TA, 4), ("q16", 0, 128), pc(P16), None, OP.is_equal)
+    quant("qc", 128, 260, "ta", ON)
+    quant("qc", 260, 388, "ta", EO)
+    copy("dup", ("qc", 0, "qc", 128, 128))
+    for b in range(2):
+        memset(("tb", 256 + b, 768, 4), 1.0)
+    ts(("f0", 0, 128), ("q16", 0, 128), pc(P16), float(BX), OP.is_equal, OP.mult)
+    ts(("f1", 0, 128), ("q16", 0, 128), pc(P16), None, OP.is_gt)
+    tt(("tb", 258, 768, 4), ("f0", 0, 128), ("f1", 0, 128), OP.add)
+    lin(("tb", 259, 768, 4), ("tb", 258, 768, 4), None, None)
+    quant("qwa", 0, 128, "tb", 256)
+    memset(("tb", 0, 256), 0.0)
+    memset(("sg", 0, 512, 2), 1.0)
+    memset(("rm", 256, 272), -2.0 * FAR)
+    memset(("dm", 0, 104), 0.0)
+    ts(("dm", 0, 96, 2), ("qrow", 0, 48), pc(PF), 16.0, OP.is_equal, OP.mult)
+    ts(("dm", 97, 103, 2), ("k16", 0, 3), pc(PH), 16.0, OP.is_equal, OP.mult)
+    lin(("dmn", 0, 104), ("dm", 0, 104), 61.5, -1000.0)
+    lin(("q16m", 0, 128), ("q16", 0, 128), None, -16.0)
+    ts(("ut", 0, 48), ("qrow", 0, 48), pc(PF), 0.5, OP.is_ge, OP.mult)
+    ts(("jj", 0, 16), ("k16", 0, 16), pc(P16), float(BC), OP.add, OP.add)
+    ts(pc(G16), pc(PF), 16.0, 32.0, OP.is_ge, OP.mult)
+    ts(pc(LT48), pc(PF), 48.0, None, OP.is_lt)
+    ts(pc(D0), pc(G16), float(BM), pc(LT48), OP.add, OP.mult)
+    ts(pc(D1), pc(PF), pc(G16), pc(LT48), OP.subtract, OP.mult)
+    ts(("pc", NB, NB + 3), ("k16", 0, 3), pc(P16), 0.5, OP.add, OP.add)
 
-    def u_tile(t):
+    for b in range(2):
+        ts(("up0", b, 1024, 4), ("ta", NEG, NEG + 256), ("us", b, b + 1), None, OP.mult)
+    for b in range(2, 4):
+        lin(("up0", 512 + b, 1024, 4), on(128), 0.0, ("us", b, b + 1), "a")
+        ts(("up0", b, 512, 4), on(128), ("us", b, b + 1), -1.0, OP.mult, OP.mult)
+    quant("qu0", 0, 256, "up0", 0)
+    quant("ca0", 0, 128, "cb", 0)
+    quant("ca0", 128, 256, "cb", 512)
+    lin(("usf", 0, 12), ("us", 0, 12), None, None, "a")
+    for t in range(1, R):
         for b in range(4):
-            act(("up%d" % t, b, 512, 4), ("zt", 0, 128), AF.Identity, bias=("us", 4 * t + b, 4 * t + b + 1))
-        act(("up%d" % t, 512, 1024), ("up%d" % t, 0, 512), AF.Copy, scale=-1.0)
+            lin(("up%d" % t, b, 1024, 4), ("ta", NEG, NEG + 256), ("usf", 4 * t + b, 4 * t + b + 1), None, "a")
+        quant("qu%d" % t, 0, 256, "up%d" % t, 0)
+    quant("qw", 0, 128, "wb", 0)
+    copy("cw0", ("w0", K, "ca0", 0, 128 - K))
+    copy("cw1", ("w1", K, "ca0", 0, 128 - K), ("w2", K, "ca0", 0, 128 - K))
 
     snd = [0]
-
-    def tg_count(t):
-        ts(c1(CB), ("p0", 0, 1), -1.0, 0.5, OP.mult, OP.add)
-        act(("s6", 0, 256), ("cum%d" % t, 0, 256), AF.Sign, bias=c1(CB), acc=c1(SS))
-
-    def tg_flags(t):
-        ts(c1(FL), c1(EEN + t), 0.5, None, OP.is_gt)
-        ts(c1(PP), c1(POSN + t), 129.0, c1(FL), OP.add, OP.mult)
-        ts(c1(H1), c1(FL), -0.5, 0.5, OP.mult, OP.add)
-        ts(c1(FLP), c1(PP), -129.0, None, OP.add)
-
-    def tg_out(t):
-        ts(("tgc", t, t + 1), c1(SS), c1(H1), c1(FLP), OP.mult, OP.add)
-        dma("s", [(T.tg[t:t + 1, :], T.tgc[0:48, t:t + 1])], "tg%d" % t, regs(("tgc", t, t + 1)), [])
-
     for t in range(R):
         ca, W, B, sl = "ca%d" % t, "w%d" % t, "b%d_" % t, "sl%d" % t
-        C0, C1 = (ca, 0, 128), (ca, 128, 256)
-        UP, UN = ("qu%d" % t, 0, 128), ("qu%d" % t, 128, 256)
-        cum = "cum%d" % t
+        C0, C1, C = (ca, 0, 128), (ca, 128, 256), (ca, 0, P)
+        UN, UP = ("qu%d" % t, 0, 128), ("qu%d" % t, 128, 256)
         o = 32 * t
         POS, EE = POSN + t, EEN + t
-        MG = 720
-
-        def mg(b):
-            return ("zb2", MG + b, MG + 64, 4)
 
         mm("p0", C0, UP, True, False)
         mm("p0", UN, C0, False, True)
@@ -341,40 +344,18 @@ def rank_program(g, core, T, topo):
         mm("p1", UN, C1, False, True)
         mm("p3", C1, UP, False, True)
         mm("p2", UN, C1, False, True)
-        dma("s", [(T[B][:, 0:P].bitcast(dt.uint8), T[ca][:, 0:P].bitcast(dt.uint8)), (T[B + "s"][:, 0:P], T[ca + "s"][:, 0:P])],
-            "cp%d" % t, regs((ca, 0, P), (ca + "s", 0, P)), regs((B, 0, P), (B + "s", 0, P)))
-        tt(("b0", 0, 128), ("p0", 0, 128), ("tri", 0, 128), OP.is_gt)
-        if t == 0:
-            ts(pc(G16), pc(PF), 16.0, 32.0, OP.is_ge, OP.mult)
-            ts(pc(LT48), pc(PF), 48.0, None, OP.is_lt)
-        scan(("e0", 0, 128), ("b0", 0, 128), ("b0", 0, 128), 0.0, OP.add, OP.add)
-        if t == 0:
-            for c in range(3):
-                ts(pc(NB + c), pc(P16), -1.0, -16.0 * c - 0.5, OP.mult, OP.add)
-        tt(("b1", 0, 128), ("p1", 0, 128), ("tri", 0, 128), OP.is_gt)
+        copy("cp%d" % t, (B, BC, ca, 0, P))
+        for b in range(2):
+            tt(("b%d" % b, 0, 128), ("p%d" % b, 0, 128), ("tri", 0, 128), OP.is_gt)
+            scan(("e%d" % b, 0, 128), ("b%d" % b, 0, 128), ("b%d" % b, 0, 128), 32.0, OP.add, OP.add)
         act(("s1", 0, 128), ("p3", 0, 128), AF.Sign, bias=TINY, acc=c1(ASUM + 1))
         act(("s0", 0, 128), ("p2", 0, 128), AF.Sign, bias=-TINY, acc=c1(ASUM))
-        if t == 0:
-            ts(("rd", 0, 128), ("qrow", 0, 128), pc(PF), 512.0, OP.not_equal, OP.mult)
-        scan(("e1", 0, 128), ("b1", 0, 128), ("b1", 0, 128), 0.0, OP.add, OP.add)
-        for b in (1, 0):
-            ts(("h", b, 384, 4), ("r2", 0, 96), c1(ASUM + b), ("e%d" % b, 127, 128), OP.subtract, OP.is_equal)
-        quant("qh", 0, 128, "h", 0, 512)
-        act(("col", NH, NH + 2), ("col", ASUM, ASUM + 2), AF.Copy, scale=-1.0, bias=-32.0)
-        mm("p0", WLH, ("qh", 0, 128), True, False)
-        mm("p0", WLL, ("qh", 0, 128), False, True)
-        if t == 0:
-            for b in range(4):
-                ts(("cb2", b, 512, 4), ("q16", 0, 128), pc(P16), None, OP.is_equal)
-            memset(("dm", 0, 80), 0.0)
-        else:
-            quant(W, WY, WN, "zt", 0, 832)
+        for b in range(2):
+            ts(("td", b, 384, 2), ("r2", 0, 192), c1(ASUM + b), ("e%d" % b, 127, 128), OP.subtract, OP.is_equal)
+        quant("qh", 0, 128, "td", 0)
+        mm("p0", WL, QH)
         op("v", lambda q: q.transpose(T.tr[:, 0:96], T.p0[:, 0:96]), regs(("p0", 0, 96)), regs(("tr", 0, 96)))
-        if t == 0:
-            ts(pc(D1), pc(PF), pc(G16), pc(LT48), OP.subtract, OP.mult)
         vcopy(("off", o, o + 3), ("tr", 0, 96, 32))
-        if t == 0:
-            ts(pc(D0), pc(G16), float(BM + 80), pc(LT48), OP.add, OP.mult)
         pick(sl, 0, K, ca, P, o, o + 3)
         dst = T.cores[rank ^ (1 << t)]
         rid, pid = topo.addr(dst)[:2]
@@ -388,130 +369,69 @@ def rank_program(g, core, T, topo):
         send(T[W + "s"][:, 0:K], T[sl + "s"][:, 0:K], mask[1], regs((sl + "s", 0, K)), regs((W + "s", 0, K)),
              (arr, n), pid, rid)
         snd[0] += n
-        if t == 0:
-            iota(("zb2", 0, 720), [[0, 720]], 0, 0)
-            iota(("zb1", 0, 512), [[0, 512]], 0, 0)
-            quant("qc1", 384, 512, "wf", 0, 512)
-        for b in range(2):
-            ts(("h2", 512 * b + b, 512 * b + 512, 4), ("rd", 0, 128), ("e%d" % b, 127, 128), c1(NH + b), OP.add, OP.is_lt)
-        if t == 0:
-            ts(("dm", 0, 48), ("qrow", 0, 48), pc(PF), 16.0, OP.is_equal, OP.mult)
-            ts(("dm", 64, 67), ("k16", 0, 3), pc(PH), 16.0, OP.is_equal, OP.mult)
-        quant("qh2", 0, 256, "h2", 0, 1024)
-        mm("p1", W1, ("qh2", 0, 256))
-        mm("p2", WF, ("qh2", 0, 256), True, False)
-        if t == 0:
-            ts(pc(NA), pc(PF), -1.0, -0.5, OP.mult, OP.add)
-            ts(pc(D2), pc(G16), float(BX), pc(LT48), OP.add, OP.mult)
-            ts(("dmn", 0, 80), ("dm", 0, 80), 61.5, -1000.0, OP.mult, OP.add)
-            quant("qc2", 0, 256, "cb2", 0, 1024)
-        else:
-            mm("p0", ("qct", 0, 128), W1)
-            tg_flags(t - 1)
-        scan((cum, 0, 256), ("p1", 0, 256), ("zt", 0, 256), 0.0, OP.add, OP.add)
-        if t == 0:
-            u_tile(1)
-        act(("s3", 0, 16), (cum, 15, 256, 16), AF.Sign, bias=pc(NA), acc=c1(HS))
-        act(("s2", 0, 256), (cum, 0, 256), AF.Sign, bias=pc(NA), acc=c1(LS))
-        if t == 0:
-            for b in range(4):
-                quant("qc3", 128 * b, 128 * b + 128, "eb", 4 - b, 516 - b)
-            quant(W, WY, WN, "zt", 0, 832)
-        else:
-            tg_count(t - 1)
-        ts(c1(T8), c1(HS), 8.0, None, OP.mult)
-        for b in range(2, 4):
-            ts(mg(b), ("kr2", 0, 16), c1(HS), None, OP.is_equal)
-        ts(c1(LO_F), c1(LS), -0.5, c1(T8), OP.mult, OP.add)
-        if t == 2:
-            quant("qw", 0, 128, "wb", 0, 512)
-        ts(("sg", 2, 512, 4), ("q16", 0, 128), c1(LO_F), pc(D2), OP.is_equal, OP.mult)
-        ts(("sg", 3, 512, 4), ("q16", 0, 128), c1(LO_F), pc(D1), OP.is_equal, OP.mult)
-        if t == 1:
-            u_tile(2)
-        AS, TS = (W, 0, 128), (W, WT, WT + 128)
-        mm("p2", AS, (ca, 0, P), False, True)
+        for out, rows, b in ((("h2", 0, 512, 2), ("rd", 0, 256), 0), (("h2", 512, 1088, 2), ("rd", 288, 576), 0),
+                             (("h2", 513, 1088, 2), ("rd", 0, 288), 1)):
+            ts(out, rows, c1(ASUM + b), ("e%d" % b, 127, 128), OP.subtract, OP.is_gt)
+        quant("qh2", 0, 272, "h2", 0)
+        mm("p2", WF, ("qh2", 0, P), True, False)
+        mm("p1", WA, ("qh2", 144, 272))
+        AS, TS = (W, 0, 128), (B, 0, 128)
+        mm("p2", AS, C, False, True)
         for b in range(4):
             mm("p%d" % (4 + b), EB[b], AS, True, False)
-        scan(("rm", 0, 256), ("p2", 0, 256), ("zt", 0, 256), -2.0 * FAR, OP.max, OP.add)
+        scan(("rm", 0, 256), ("p2", 0, 256), on(256), -2.0 * FAR, OP.max, OP.mult)
+        act(("s4", 0, 17), ("rm", 15, 272, 16), AF.Sign, scale=-1.0, bias=("rm", 255, 256), acc=c1(HI))
         act(("s5", 0, 256), ("rm", 0, 256), AF.Sign, scale=-1.0, bias=("rm", 255, 256), acc=c1(POS))
-        ts(("s4", 0, 17), ("rm", 15, 272, 16), ("rm", 255, 256), None, OP.is_lt)
-        if t == 0:
-            ts(("ut", 0, 48), ("qrow", 0, 48), pc(PF), 0.5, OP.is_ge, OP.mult)
-            ts(("jj", 0, 16), ("k16", 0, 16), pc(P16), None, OP.add)
-        red(c1(HI), ("s4", 0, 17), OP.add)
-        if t == 0:
-            ts(("zb2", 258, 268, 4), ("dm", 64, 67), -1.0, None, OP.mult)
-        else:
-            tg_out(t - 1)
-        ts(("dh", 0, 68), ("dmn", 0, 68), c1(HI), 16.0, OP.mult, OP.add)
-        ts(("zb2", 0, 272, 4), ("dm", 0, 68), c1(HI), None, OP.mult)
-        ts(("zb2", 1, 272, 4), ("dh", 0, 68), c1(POS), 0.0, OP.add, OP.max)
-        ts(c1(H16), c1(HI), -16.0, c1(POS), OP.mult, OP.add)
-        quant("qd", 0, 128, "zb2", 0, 512)
-        mm("p1", WO, ("qd", 0, 128))
-        mm("p0", WE, ("qd", 0, 128), True, False)
-        mm("p0", ("qd", 0, 128), W1, False, True)
-        for c in range(3):
-            act(("x%d" % c, 0, 256), (cum, 0, 256), AF.Sign, bias=pc(NB + c), acc=c1(LSUM + c))
-        ts(("sg", 0, 512, 4), ("q16m", 0, 128), c1(H16), pc(D0), OP.is_equal, OP.mult)
-        ts(("sg", 1, 512, 4), ("q16m", 0, 128), c1(H16), pc(D1), OP.is_equal, OP.mult)
-        if t == 0:
-            for c in range(3):
-                ts(pc(AC + c), pc(P16), 16.0 * c, None, OP.add)
-        vcopy(("off", o + 4, o + 7), ("p1", 64, 67))
-        quant("qsg", 0, 128, "sg", 0, 512)
-        pick(W, WT, WT + K, ca, P, o + 4, o + 7)
+        lin(("dh", 0, 104), ("dmn", 0, 104), c1(HI), 16.0)
+        lin(("ta", 0, NEG, 2), ("dm", 0, 104), c1(HI), None)
+        ts(("ta", 1, NEG, 2), ("dh", 0, 104), c1(POS), 0.0, OP.add, OP.max)
+        lin(c1(H16), c1(HI), -16.0, c1(POS))
+        quant("qd", 0, 128, "ta", 0)
+        mm("p0", WEO, QD, True, False)
+        mm("p0", QD, W48, False, True)
+        ts(("sg", 1, 512, 4), ("q16m", 0, 128), c1(H16), pc(D0), OP.is_equal, OP.mult)
+        ts(("sg", 3, 512, 4), ("q16m", 0, 128), c1(H16), pc(D1), OP.is_equal, OP.mult)
+        quant("qsg", 0, 128, "sg", 0)
+        red(c1(EE), ("p0", 0, 48), OP.min, True)
+        ts(("off", o + 4, o + 7), ("p0", 48, 51), -16.0, None, OP.add)
+        pick(B, 0, K, ca, P, o + 4, o + 7)
         for b in range(4):
             mm("p%d" % (4 + b), EB[b], TS, False, True)
-        red(c1(EE), ("p0", 0, 48), OP.min, True)
-        ts(("zb1", 0, 192, 4), ("ut", 0, 48), c1(EE), None, OP.is_gt)
-        ts(("off", o + 8, o + 11), ("col", LSUM, LSUM + 3), -0.5, 128.0, OP.mult, OP.add)
-        ts(mg(0), ("kr", 0, 16), c1(HI), c1(EE), OP.is_equal, OP.min)
-        quant("qct", 0, 128, "zb1", 0, 512)
-        ts(mg(1), ("kr", 0, 16), c1(HI), c1(EE), OP.is_equal, OP.min)
-        pick(W, WY, WY + K, ca, P, o + 8, o + 11)
-        quant("qmg", 0, 128, "zb2", 272, 784)
-        mm("p3", W1, ("qct", 0, 128))
-        mm("p1", W1, ("qct", 0, 128))
-        mm("p2", ("qsg", 0, 128), ("qmg", 0, 128))
-        for b in range(2):
-            act(("zb1", 512 + b, 704, 4), ("p%d" % (4 + b), 0, 48), AF.Copy, scale=0.5)
-        for b in range(2, 4):
-            ts(("zb1", 512 + b, 704, 4), ("p%d" % (4 + b), 0, 48), 0.5, None, OP.mult)
-        for c in range(2):
-            act(("y%d" % c, 0, 96), ("p3", 0, 96), AF.Sign, bias=pc(NB + c), acc=c1(SX + c))
-        ts(("b2", 0, 48), ("p1", 0, 48), pc(AC + 2), None, OP.is_le)
+        ts(("tb", 0, 192, 4), ("ut", 0, 48), c1(EE), -1.0, OP.is_gt, OP.mult)
+        ts(("tb", 193, 256, 2), ("kr", 0, 32), c1(HI), c1(EE), OP.is_equal, OP.min)
+        quant("qz", 0, 128, "tb", 0)
+        mm("p3", W1, QZ)
+        mm("p2", QS, QZ)
+        for b in range(4):
+            lin(("tc", b, 192, 4), ("p%d" % (4 + b), 0, 48), 0.5, None, "a")
+        quant(B, BM, BM + 128, "tc", 0)
         for c in range(3):
-            ts(c1(KX + c), ("p1", 47, 48), pc(AC + c), pc(AC + c), OP.is_le, OP.mult)
-        red(c1(SX + 2), ("b2", 0, 48), OP.add)
-        tt(("go", 0, 16), ("p2", 112, 128), ("jj", 0, 16), OP.max)
-        for c in range(2):
-            ts(("off", o + 12 + c, o + 13 + c), c1(SX + c), -0.5, c1(KX + c), OP.mult, OP.add)
-        vcopy(("off", o + 16, o + 32), ("go", 0, 16))
-        ts(("off", o + 14, o + 15), c1(SX + 2), c1(KX + 2), None, OP.add)
-        if t == R - 1:
-            mm("p0", ("qct", 0, 128), W1)
-        quant(B, BM, BN, "zb1", 192, 704)
-        pick(B, BX, BX + K, W, WX, o + 12, o + 15)
+            act(("y%d" % c, 0, 48), ("p3", 0, 48), AF.Sign, bias=pc(NB + c), acc=c1(SX + c))
+        ts(("off", o + 8, o + 11), ("col", SX, SX + 3), 0.5, 24.0, OP.mult, OP.add)
+        pick(B, BX, BX + K, W, 128, o + 8, o + 11)
+        ts(("go", 0, 16), ("p1", 112, 128), ("p2", 47, 48), float(BX), OP.add, OP.is_lt)
+        tt(("go", 16, 32), ("p1", 112, 128), ("go", 0, 16), OP.mult)
+        tt(("go", 32, 48), ("p2", 48, 64), ("jj", 0, 16), OP.max)
+        tt(("go", 48, 64), ("go", 16, 32), ("go", 32, 48), OP.max)
+        vcopy(("off", o + 16, o + 32), ("go", 48, 64))
         nx = "ca%d" % (t + 1)
-        if t < R - 1:
-            quant("qu%d" % (t + 1), 0, 128, "up%d" % (t + 1), 0, 512)
-        else:
-            tg_count(t)
         pick(nx, 0, 128, B, BN, o + 16, o + 24)
-        if t < R - 1:
-            quant("qu%d" % (t + 1), 128, 256, "up%d" % (t + 1), 512, 1024)
         pick(nx, 128, 256, B, BN, o + 24, o + 32)
+        pt = "p4" if t < R - 1 else "p0"
+        mm(pt, W1, ("qh2", 0, P), True, False)
+        mm(pt, QZ, W256, False, True)
+        act(("s6", 0, 256), (pt, 0, 256), AF.Sign, bias=0.5, acc=c1(SS + t))
+        lin(c1(UU + t), c1(SS + t), 0.5, -129.0, "a")
+        act(c1(MF + t), c1(EE), AF.Relu, bias=512.0, scale=-512.0)
+        ts(("tgc", t, t + 1), c1(POS), c1(MF + t), c1(UU + t), OP.subtract, OP.max)
+        dma("s", [(T.tg[t:t + 1, :], T.tgc[0:48, t:t + 1])], "tg%d" % t, regs(("tgc", t, t + 1)), [])
 
     for i in range(2):
         a, b = 128 * i, 128 * i + 128
         dma("s", [(T.oc[:, 4 * a:4 * b], T.ca3[:, a:b].bitcast(dt.uint8))], "outs", regs(("ca3", a, b)), [])
         mm("p%d" % (1 + 2 * i), ("qw", 0, 128), ("ca3", a, b))
     dma("a", [(T.osc[4 * k:4 * k + 4, 0:P], T.ca3s[32 * k:32 * k + 4, 0:P]) for k in range(4)], "osc", regs(("ca3s", 0, P)), [])
-    tg_flags(R - 1)
     lin(("yo", 0, 128), ("p1", 0, 128), None, None)
-    tg_out(R - 1)
     lin(("yo", 128, 256), ("p3", 0, 128), None, None)
     for a in (0, 128):
         dma("s", [(T.y[:, a:a + 128], T.yo[:, a:a + 128])], "outs", regs(("yo", a, a + 128)), [])

from concourse.mybir import dt, AluOpType, AxisListType, ActivationFunctionType

OP = AluOpType
AF = ActivationFunctionType
P, K, R = 256, 48, 3
BC, BX, BM, BN = 48, 320, 384, 432
TINY = 2.0 ** -100
FAR = 2.0 ** 75
NEG, ON, ZR, EO, TA = 208, 336, 848, 864, 1376

SCRATCH = {}
for _n, _w in (("cb", 1024), ("us", 16), ("wb", 512), ("up0", 1024), ("up1", 1024), ("up2", 1024), ("ta", TA), ("tb", 768),
               ("tc", 708), ("td", 896), ("wf", 512), ("h2", 1088), ("rd", 576), ("r2", 192), ("qrow", 128), ("q16", 128),
               ("q16m", 128), ("kr", 32), ("dm", 104), ("dmn", 104), ("dh", 104), ("ut", 48), ("b0", 128), ("b1", 128),
               ("tri", 128), ("sg", 512), ("f0", 128), ("f1", 128), ("s0", 128), ("s1", 128),
               ("s4", 32), ("s5", 256), ("s6", 256), ("y0", 48), ("y1", 48), ("y2", 48)):
    SCRATCH[_n] = ("sbuf", [128, _w], "bfloat16")
for _n, _w in (("k16", 16), ("jj", 16), ("pc", 16), ("usf", 16), ("tr", 96), ("rm", 272), ("go", 64), ("yo", 256),
               ("col", 32), ("tgc", 16), ("e0", 128), ("e1", 128)):
    SCRATCH[_n] = ("sbuf", [128, _w], "float32")
SCRATCH["pi"] = ("sbuf", [128, 8], "int32")
SCRATCH["off"] = ("sbuf", [128, 96], "uint16")
_codes = [("qu0", 256), ("qu1", 256), ("qu2", 256), ("qc", 388), ("qwl", 128), ("qwa", 128), ("qwf", 128), ("qe", 512),
          ("qh", 128), ("qh2", 272), ("qd", 128), ("qz", 128), ("qsg", 128), ("qw", 128), ("ca3", 256)]
for _t in range(R):
    _codes += [("ca%d" % _t, P), ("w%d" % _t, 128), ("b%d_" % _t, 512), ("sl%d" % _t, K)]
for _n, _w in _codes:
    SCRATCH[_n] = ("sbuf", [128, _w], "float8_e4m3fn_x4")
    SCRATCH[_n + "s"] = ("sbuf", [128, _w], "uint8")
for _i in range(8):
    SCRATCH["p%d" % _i] = ("psum", [128, 512], "float32")

SEMAPHORES = ["sv", "sa", "st", "sg", "ldc0", "ldc1", "ldu", "ldw", "snd", "arr0", "arr1", "arr2", "cp0", "cp1", "cp2",
              "cw0", "cw1", "dup", "tg0", "tg1", "tg2", "outs", "osc"]

ORDER = [60,4,0,5,1,12,14,15,29,30,11,16,36,9,22,42,35,40,18,17,34,77,21,73,72,2,75,74,10,79,6,76,78,81,80,3,38,19,95,20,59,32,23,96,8,7,99,100,64,39,93,97,104,106,105,87,94,102,89,98,101,83,109,107,108,13,110,111,31,103,112,122,85,113,37,120,114,51,115,44,116,67,24,82,68,71,41,45,53,90,88,70,46,84,69,52,121,62,47,43,54,117,55,118,119,28,33,26,123,27,124,126,25,57,48,91,61,63,131,50,130,128,58,56,132,125,134,133,65,136,137,135,138,127,142,129,141,139,140,92,144,49,145,143,153,152,146,154,147,148,66,86,156,155,149,168,157,162,170,163,158,169,150,151,159,164,160,171,165,161,172,181,166,167,177,173,174,175,178,184,185,176,193,179,186,188,192,189,191,198,187,195,190,194,197,196,199,200,180,201,210,202,203,182,204,206,205,207,209,211,212,208,213,215,220,221,223,224,222,225,226,227,228,230,231,232,229,233,234,219,242,236,214,217,218,241,235,216,238,243,245,244,239,247,252,240,257,259,258,248,249,251,260,253,237,246,254,256,270,266,267,250,261,255,262,264,263,265,273,274,275,268,282,277,278,284,283,280,287,285,288,276,279,286,289,269,290,300,291,183,292,271,293,294,298,281,296,295,299,301,303,302,297,304,309,310,308,312,313,311,314,315,316,317,318,307,319,320,321,322,305,323,331,330,355,325,306,324,327,336,359,332,334,333,346,348,329,342,347,338,349,326,328,340,356,341,335,343,337,350,272,344,345,339,357,351,352,363,362,353,358,364,354,365,367,360,366,369,361,368,370]
OTHER = {17,19,20,21,22,55,63,64,135,158,159,180,247,248,249,269,338,358}


def scheduler(g, T):
    queue = {"v": g.vector, "a": g.scalar, "t": g.tensor, "g": g, "s": g.sync}
    count = {"v": 0, "a": 0, "t": 0, "g": 0}
    seen = {k: {} for k in "vatgs"}
    clock = {}
    wr, rd, total = {}, {}, {}

    def need(e, ds):
        best = {}
        for s, v in ds:
            if seen[e].get(s, 0) < v:
                best[s] = max(best.get(s, 0), v)
        for s in list(best):
            for s2 in best:
                if s2 != s and clock.get((s2, best[s2]), {}).get(s, 0) >= best[s]:
                    del best[s]
                    break
        for s, v in best.items():
            queue[e].wait_ge(T.sem[s], v)
            for k2, v2 in clock.get((s, v), {}).items():
                seen[e][k2] = max(seen[e].get(k2, 0), v2)
            seen[e][s] = max(seen[e].get(s, 0), v)

    def hit(a, b):
        if a[1] >= b[2] or b[1] >= a[2]:
            return False
        return not (a[3] == b[3] and a[3] > 1 and (a[1] - b[1]) % a[3])

    def deps(reads, writes):
        d = [ev for r in reads for (q, ev) in wr.get(r[0], []) if hit(r, q)]
        return d + [ev for w in writes for (q, ev) in wr.get(w[0], []) + rd.get(w[0], []) if hit(w, q)]

    def note(reads, writes, ev):
        for r in reads:
            rd.setdefault(r[0], []).append((r, ev))
        for w in writes:
            def old(q):
                return q[1] >= w[1] and q[2] <= w[2] and (w[3] == 1 or (w[3] == q[3] and (q[1] - w[1]) % w[3] == 0))
            wr[w[0]] = [x for x in wr.get(w[0], []) if not old(x[0])] + [(w, ev)]
            rd[w[0]] = [x for x in rd.get(w[0], []) if not old(x[0])]

    def op(e, fn, reads, writes):
        bank = [ev for r in reads if r[0][1:].isdigit() and r[0][0] == "p" for (q, ev) in rd.get(r[0], []) if ev[0] != "s" + e]
        need(e, deps(reads, writes) + bank)
        count[e] += 1
        ev = ("s" + e, count[e])
        fn(queue[e]).then_inc(T.sem[ev[0]], 1)
        clock[ev] = dict(seen[e])
        note(reads, writes, ev)

    def dma(e, pairs, sem, reads, writes):
        need(e, deps(reads, writes))
        for out, in_ in pairs:
            queue[e].dma_start(out, in_).then_inc(T.sem[sem], 16)
            total[sem] = total.get(sem, 0) + 16
        ev = (sem, total[sem])
        clock[ev] = dict(seen[e])
        note(reads, writes, ev)

    return op, dma, need, deps, note, count, total


def rank_program(g, core, T, topo):
    rank = T.rank_of(core)
    if rank is None:
        return
    op0, dma0, need, deps, note, count, total = scheduler(g, T)
    items = []

    def op(e, fn, reads, writes, alt=None, acc=None):
        items.append(("op", e, fn, reads, writes, alt, acc))

    def dma(e, pairs, sem, reads, writes):
        items.append(("dma", e, pairs, reads, writes, None, sem))

    def send(out, in_, mask, reads, writes, ev, pid, rid):
        def fn():
            need("g", deps(reads, []))
            g.remote_dma(out, in_, T.sem[ev[0]], T.sem.snd, pid, rid, mask)
            note([], writes, ev)
        items.append(("send", "g", fn, reads, writes, None, ev))

    def issue():
        for i in (ORDER or range(len(items))):
            kind, e, fn, reads, writes, alt, x = items[i]
            if kind == "send":
                fn()
            elif kind == "dma":
                dma0(e, fn, x, reads, writes)
            else:
                if i in OTHER:
                    e, fn = alt
                op0(e, fn, reads, writes)
                if x:
                    note([], x, ("st", count["t"]))

    def V(x):
        return T[x[0]][:, x[1]:x[2]:x[3]] if len(x) == 4 else T[x[0]][:, x[1]:x[2]]

    def opnd(x):
        return V(x) if isinstance(x, tuple) else x

    def regs(*xs):
        out = []
        for x in xs:
            if isinstance(x, tuple):
                if x[0][0] == "p" and x[0][1:].isdigit():
                    out.append((x[0], 0, 512, 1))
                else:
                    out.append((x[0], x[1], x[2], x[3] if len(x) == 4 else 1))
        return out

    def lin(out, a, scale, bias, e="v"):
        kw = {k: opnd(x) for k, x in (("scale", scale), ("bias", bias)) if x is not None}
        fa = AF.Identity if isinstance(scale, tuple) or isinstance(bias, tuple) else AF.Copy
        args = [(opnd(x), o) for x, o in ((scale, OP.mult), (bias, OP.add)) if x is not None] or [(1.0, OP.mult)]

        def fv(q):
            if len(args) == 1:
                return q.tensor_scalar(V(out), V(a), args[0][0], None, args[0][1])
            return q.tensor_scalar(V(out), V(a), args[0][0], args[1][0], OP.mult, OP.add)
        both = {"v": fv, "a": lambda q: q.activation(V(out), V(a), fa, **kw)}
        o = "a" if e == "v" else "v"
        op(e, both[e], regs(a, scale, bias), regs(out), (o, both[o]))

    def memset(x, c):
        op("v", lambda q: q.memset(V(x), c), [], regs(x))

    def ts(out, in0, s1, s2, op0, op1=None):
        if op1 is None:
            op("v", lambda q: q.tensor_scalar(V(out), V(in0), opnd(s1), None, op0), regs(in0, s1), regs(out))
        else:
            op("v", lambda q: q.tensor_scalar(V(out), V(in0), opnd(s1), opnd(s2), op0, op1), regs(in0, s1, s2), regs(out))

    def tt(out, a, b, o):
        op("v", lambda q: q.tensor_tensor(V(out), V(a), V(b), o), regs(a, b), regs(out))

    def vcopy(out, a):
        op("v", lambda q: q.tensor_copy(V(out), V(a)), regs(a), regs(out))

    def red(out, a, o, absv=False):
        kw = {"apply_absolute_value": True} if absv else {}
        op("v", lambda q: q.tensor_reduce(V(out), V(a), AxisListType.X, o, **kw), regs(a), regs(out))

    def scan(out, a, b, init, op0, op1):
        op("v", lambda q: q.tensor_tensor_scan(V(out), V(a), V(b), init, op0, op1), regs(a, b), regs(out))

    def act(out, a, fn, bias=None, scale=None, acc=None):
        kw = {}
        if bias is not None:
            kw["bias"] = opnd(bias)
        if scale is not None:
            kw["scale"] = opnd(scale)
        if acc is not None:
            kw["accum_out"] = V(acc)
        op("a", lambda q: q.activation(V(out), V(a), fn, **kw), regs(a, bias, scale), regs(out, acc))

    def quant(qn, a, b, src, f):
        e = f + 4 * (b - a)
        op("v", lambda q: q.quantize_mx(T[qn][:, a:b], T[qn + "s"][:, a:b], T[src][:, f:e]),
           regs((src, f, e)), regs((qn, a, b), (qn + "s", a, b)))

    def mm(pn, l, r, start=True, stop=True):
        n = r[2] - r[1]
        reads = regs(l, r, (l[0] + "s", l[1], l[2]), (r[0] + "s", r[1], r[2]))
        op("t", lambda q: q.matmul_mx(T[pn][:, 0:n], T[l[0]][:, l[1]:l[2]], T[l[0] + "s"][:, l[1]:l[2]],
                                      T[r[0]][:, r[1]:r[2]], T[r[0] + "s"][:, r[1]:r[2]], start, stop),
           reads, regs((pn, 0, 512)) if start else [], None, None if start else regs((pn, 0, 512)))

    def pick(dst, a, b, src, n, o0, o1):
        off = ("off", o0, o1)
        op("v", lambda q: q.tensor_copy(T[dst][:, a:b].bitcast(dt.uint32), T[src][:, 0:n].bitcast(dt.uint32).indirect(V(off))),
           regs((src, 0, n), off), regs((dst, a, b)))
        op("a", lambda q: q.activation(T[dst + "s"][:, a:b], T[src + "s"][:, 0:n].indirect(V(off)), AF.Copy),
           regs((src + "s", 0, n), off), regs((dst + "s", a, b)),
           ("v", lambda q: q.tensor_copy(T[dst + "s"][:, a:b], T[src + "s"][:, 0:n].indirect(V(off)))))

    def copy(sem, *moves):
        pairs, reads, writes = [], [], []
        for dst, a, src, f, n in moves:
            pairs += [(T[dst][:, a:a + n].bitcast(dt.uint8), T[src][:, f:f + n].bitcast(dt.uint8)),
                      (T[dst + "s"][:, a:a + n], T[src + "s"][:, f:f + n])]
            reads += regs((src, f, f + n), (src + "s", f, f + n))
            writes += regs((dst, a, a + n), (dst + "s", a, a + n))
        dma("s", pairs, sem, reads, writes)

    def iota(out, pattern, base, cm, small=True):
        kw = {"allow_small_or_imprecise_dtypes": True} if small else {}
        op("g", lambda q: q.iota(V(out), pattern, base, cm, **kw), [], regs(out))

    def c1(i):
        return ("col", i, i + 1)

    def pc(i):
        return ("pc", i, i + 1)

    def on(n):
        return ("ta", ON, ON + n)

    PF, P16, PH, PH1, G16, LT48, D0, D1, NB = 0, 1, 2, 3, 4, 5, 6, 7, 8
    ASUM, HI, H16, POSN, EEN, SX, SS, UU, MF = 0, 2, 3, 4, 8, 12, 16, 20, 24
    W1, W256, W48, WEO = ("qc", 128, 256), ("qc", 0, 256), ("qc", 208, 336), ("qc", 260, 388)
    WL, WA, WF = ("qwl", 0, 128), ("qwa", 0, 128), ("qwf", 0, 128)
    EB = [("qe", 128 * i, 128 * i + 128) for i in range(4)]
    QH, QD, QZ, QS = ("qh", 0, 128), ("qd", 0, 128), ("qz", 0, 128), ("qsg", 0, 128)

    dma("a", [(T.us[:, 0:12], T.u[:, 0:12])], "ldu", [], regs(("us", 0, 12)))
    dma("s", [(T.cb[:, 0:512], T.c[:, 0:512])], "ldc0", [], regs(("cb", 0, 512)))
    dma("s", [(T.cb[:, 512:1024], T.c[:, 512:1024])], "ldc1", [], regs(("cb", 512, 1024)))
    dma("s", [(T.wb[:, :], T.w[:, :])], "ldw", [], regs(("wb", 0, 512)))

    iota(("pi", 0, 1), [[1, 1]], 0, 1, False)
    iota(("qrow", 0, 128), [[1, 128]], 0, 0)
    for b in range(2):
        iota(("r2", b, 192, 2), [[32, 3], [0, 2], [2, 16]], -96, 0)
    iota(("q16", 0, 128), [[0, 8], [1, 16]], 0, 0)
    iota(("k16", 0, 16), [[16, 16]], 0, 0)
    iota(("kr", 0, 32), [[1, 16], [0, 2]], 1, 0)

    memset(("ta", NEG, ON), -1.0)
    memset(on(512), 1.0)
    memset(("ta", ZR, EO), 0.0)
    ts(("pi", 1, 2), ("pi", 0, 1), 15, None, OP.bitwise_and)
    ts(("pi", 2, 3), ("pi", 0, 1), 112, None, OP.bitwise_and)
    vcopy(("pc", 0, 3), ("pi", 0, 3))
    lin(pc(PH1), pc(PH), None, 128.0)
    ts(("tri", 0, 128), ("qrow", 0, 128), pc(PF), -TINY, OP.is_lt, OP.mult)
    for b, x in enumerate((PH, PH1, P16, P16)):
        lin(("td", 384 + b, 896, 4), on(128), pc(x), None)
    quant("qwl", 0, 128, "td", 384)
    op("g", lambda q: q.affine_select(V(("tc", 192, 708)), V(on(516)), [[-1, 516]], OP.is_equal, 0.0, 3, 4),
       regs(on(516)), regs(("tc", 192, 708)))
    for b in range(4):
        quant("qe", 128 * b, 128 * b + 128, "tc", 195 - b)
    for b in range(4):
        memset(("wf", b, 512, 4), -FAR if b < 2 else 0.0)
    quant("qwf", 0, 128, "wf", 0)
    ts(("rd", 0, 256, 2), ("qrow", 0, 128), pc(PF), -512.0, OP.not_equal, OP.mult)
    ts(("rd", 1, 256, 2), ("qrow", 0, 128), pc(PF), -512.0, OP.is_le, OP.mult)
    memset(("rd", 288, 544, 2), -512.0)
    memset(("rd", 289, 544, 2), 0.0)
    for a, x in ((256, PH1), (544, PH)):
        ts(("rd", a, a + 32, 2), ("k16", 0, 16), pc(x), -512.0, OP.is_le, OP.mult)
        ts(("rd", a + 1, a + 32, 2), ("k16", 0, 16), pc(x), -512.0, OP.not_equal, OP.mult)
    memset(("h2", 1, 512, 2), 0.0)
    for b in range(2):
        ts(("ta", EO + b, TA, 4), ("qrow", 0, 128), pc(PF), -1.0, OP.is_gt, OP.mult)
        ts(("ta", EO + 2 + b, TA, 4), ("q16", 0, 128), pc(P16), None, OP.is_equal)
    quant("qc", 128, 260, "ta", ON)
    quant("qc", 260, 388, "ta", EO)
    copy("dup", ("qc", 0, "qc", 128, 128))
    for b in range(2):
        memset(("tb", 256 + b, 768, 4), 1.0)
    ts(("f0", 0, 128), ("q16", 0, 128), pc(P16), float(BX), OP.is_equal, OP.mult)
    ts(("f1", 0, 128), ("q16", 0, 128), pc(P16), None, OP.is_gt)
    tt(("tb", 258, 768, 4), ("f0", 0, 128), ("f1", 0, 128), OP.add)
    lin(("tb", 259, 768, 4), ("tb", 258, 768, 4), None, None)
    quant("qwa", 0, 128, "tb", 256)
    memset(("tb", 0, 256), 0.0)
    memset(("sg", 0, 512, 2), 1.0)
    memset(("rm", 256, 272), -2.0 * FAR)
    memset(("dm", 0, 104), 0.0)
    ts(("dm", 0, 96, 2), ("qrow", 0, 48), pc(PF), 16.0, OP.is_equal, OP.mult)
    ts(("dm", 97, 103, 2), ("k16", 0, 3), pc(PH), 16.0, OP.is_equal, OP.mult)
    lin(("dmn", 0, 104), ("dm", 0, 104), 61.5, -1000.0)
    lin(("q16m", 0, 128), ("q16", 0, 128), None, -16.0)
    ts(("ut", 0, 48), ("qrow", 0, 48), pc(PF), 0.5, OP.is_ge, OP.mult)
    ts(("jj", 0, 16), ("k16", 0, 16), pc(P16), float(BC), OP.add, OP.add)
    ts(pc(G16), pc(PF), 16.0, 32.0, OP.is_ge, OP.mult)
    ts(pc(LT48), pc(PF), 48.0, None, OP.is_lt)
    ts(pc(D0), pc(G16), float(BM), pc(LT48), OP.add, OP.mult)
    ts(pc(D1), pc(PF), pc(G16), pc(LT48), OP.subtract, OP.mult)
    ts(("pc", NB, NB + 3), ("k16", 0, 3), pc(P16), 0.5, OP.add, OP.add)

    for b in range(2):
        ts(("up0", b, 1024, 4), ("ta", NEG, NEG + 256), ("us", b, b + 1), None, OP.mult)
    for b in range(2, 4):
        lin(("up0", 512 + b, 1024, 4), on(128), 0.0, ("us", b, b + 1), "a")
        ts(("up0", b, 512, 4), on(128), ("us", b, b + 1), -1.0, OP.mult, OP.mult)
    quant("qu0", 0, 256, "up0", 0)
    quant("ca0", 0, 128, "cb", 0)
    quant("ca0", 128, 256, "cb", 512)
    lin(("usf", 0, 12), ("us", 0, 12), None, None, "a")
    for t in range(1, R):
        for b in range(4):
            lin(("up%d" % t, b, 1024, 4), ("ta", NEG, NEG + 256), ("usf", 4 * t + b, 4 * t + b + 1), None, "a")
        quant("qu%d" % t, 0, 256, "up%d" % t, 0)
    quant("qw", 0, 128, "wb", 0)
    copy("cw0", ("w0", K, "ca0", 0, 128 - K))
    copy("cw1", ("w1", K, "ca0", 0, 128 - K), ("w2", K, "ca0", 0, 128 - K))

    snd = [0]
    for t in range(R):
        ca, W, B, sl = "ca%d" % t, "w%d" % t, "b%d_" % t, "sl%d" % t
        C0, C1, C = (ca, 0, 128), (ca, 128, 256), (ca, 0, P)
        UN, UP = ("qu%d" % t, 0, 128), ("qu%d" % t, 128, 256)
        o = 32 * t
        POS, EE = POSN + t, EEN + t

        mm("p0", C0, UP, True, False)
        mm("p0", UN, C0, False, True)
        mm("p2", C0, UP, True, False)
        mm("p3", UN, C0, True, False)
        mm("p1", C1, UP, True, False)
        mm("p1", UN, C1, False, True)
        mm("p3", C1, UP, False, True)
        mm("p2", UN, C1, False, True)
        copy("cp%d" % t, (B, BC, ca, 0, P))
        for b in range(2):
            tt(("b%d" % b, 0, 128), ("p%d" % b, 0, 128), ("tri", 0, 128), OP.is_gt)
            scan(("e%d" % b, 0, 128), ("b%d" % b, 0, 128), ("b%d" % b, 0, 128), 32.0, OP.add, OP.add)
        act(("s1", 0, 128), ("p3", 0, 128), AF.Sign, bias=TINY, acc=c1(ASUM + 1))
        act(("s0", 0, 128), ("p2", 0, 128), AF.Sign, bias=-TINY, acc=c1(ASUM))
        for b in range(2):
            ts(("td", b, 384, 2), ("r2", 0, 192), c1(ASUM + b), ("e%d" % b, 127, 128), OP.subtract, OP.is_equal)
        quant("qh", 0, 128, "td", 0)
        mm("p0", WL, QH)
        op("v", lambda q: q.transpose(T.tr[:, 0:96], T.p0[:, 0:96]), regs(("p0", 0, 96)), regs(("tr", 0, 96)))
        vcopy(("off", o, o + 3), ("tr", 0, 96, 32))
        pick(sl, 0, K, ca, P, o, o + 3)
        dst = T.cores[rank ^ (1 << t)]
        rid, pid = topo.addr(dst)[:2]
        eng = topo.engines(core, dst)[:8]
        part = (eng[0::2], eng[1::2]) if t == 0 else (eng, eng)
        mask = [sum(1 << e for e in p) for p in part]
        n = len(part[0]) + len(part[1])
        arr = "arr%d" % t
        send(T[W][:, 0:K].bitcast(dt.uint8), T[sl][:, 0:K].bitcast(dt.uint8), mask[0], regs((sl, 0, K)), regs((W, 0, K)),
             (arr, n), pid, rid)
        send(T[W + "s"][:, 0:K], T[sl + "s"][:, 0:K], mask[1], regs((sl + "s", 0, K)), regs((W + "s", 0, K)),
             (arr, n), pid, rid)
        snd[0] += n
        for out, rows, b in ((("h2", 0, 512, 2), ("rd", 0, 256), 0), (("h2", 512, 1088, 2), ("rd", 288, 576), 0),
                             (("h2", 513, 1088, 2), ("rd", 0, 288), 1)):
            ts(out, rows, c1(ASUM + b), ("e%d" % b, 127, 128), OP.subtract, OP.is_gt)
        quant("qh2", 0, 272, "h2", 0)
        mm("p2", WF, ("qh2", 0, P), True, False)
        mm("p1", WA, ("qh2", 144, 272))
        AS, TS = (W, 0, 128), (B, 0, 128)
        mm("p2", AS, C, False, True)
        for b in range(4):
            mm("p%d" % (4 + b), EB[b], AS, True, False)
        scan(("rm", 0, 256), ("p2", 0, 256), on(256), -2.0 * FAR, OP.max, OP.mult)
        act(("s4", 0, 17), ("rm", 15, 272, 16), AF.Sign, scale=-1.0, bias=("rm", 255, 256), acc=c1(HI))
        act(("s5", 0, 256), ("rm", 0, 256), AF.Sign, scale=-1.0, bias=("rm", 255, 256), acc=c1(POS))
        lin(("dh", 0, 104), ("dmn", 0, 104), c1(HI), 16.0)
        lin(("ta", 0, NEG, 2), ("dm", 0, 104), c1(HI), None)
        ts(("ta", 1, NEG, 2), ("dh", 0, 104), c1(POS), 0.0, OP.add, OP.max)
        lin(c1(H16), c1(HI), -16.0, c1(POS))
        quant("qd", 0, 128, "ta", 0)
        mm("p0", WEO, QD, True, False)
        mm("p0", QD, W48, False, True)
        ts(("sg", 1, 512, 4), ("q16m", 0, 128), c1(H16), pc(D0), OP.is_equal, OP.mult)
        ts(("sg", 3, 512, 4), ("q16m", 0, 128), c1(H16), pc(D1), OP.is_equal, OP.mult)
        quant("qsg", 0, 128, "sg", 0)
        red(c1(EE), ("p0", 0, 48), OP.min, True)
        ts(("off", o + 4, o + 7), ("p0", 48, 51), -16.0, None, OP.add)
        pick(B, 0, K, ca, P, o + 4, o + 7)
        for b in range(4):
            mm("p%d" % (4 + b), EB[b], TS, False, True)
        ts(("tb", 0, 192, 4), ("ut", 0, 48), c1(EE), -1.0, OP.is_gt, OP.mult)
        ts(("tb", 193, 256, 2), ("kr", 0, 32), c1(HI), c1(EE), OP.is_equal, OP.min)
        quant("qz", 0, 128, "tb", 0)
        mm("p3", W1, QZ)
        mm("p2", QS, QZ)
        for b in range(4):
            lin(("tc", b, 192, 4), ("p%d" % (4 + b), 0, 48), 0.5, None, "a")
        quant(B, BM, BM + 128, "tc", 0)
        for c in range(3):
            act(("y%d" % c, 0, 48), ("p3", 0, 48), AF.Sign, bias=pc(NB + c), acc=c1(SX + c))
        ts(("off", o + 8, o + 11), ("col", SX, SX + 3), 0.5, 24.0, OP.mult, OP.add)
        pick(B, BX, BX + K, W, 128, o + 8, o + 11)
        ts(("go", 0, 16), ("p1", 112, 128), ("p2", 47, 48), float(BX), OP.add, OP.is_lt)
        tt(("go", 16, 32), ("p1", 112, 128), ("go", 0, 16), OP.mult)
        tt(("go", 32, 48), ("p2", 48, 64), ("jj", 0, 16), OP.max)
        tt(("go", 48, 64), ("go", 16, 32), ("go", 32, 48), OP.max)
        vcopy(("off", o + 16, o + 32), ("go", 48, 64))
        nx = "ca%d" % (t + 1)
        pick(nx, 0, 128, B, BN, o + 16, o + 24)
        pick(nx, 128, 256, B, BN, o + 24, o + 32)
        pt = "p4" if t < R - 1 else "p0"
        mm(pt, W1, ("qh2", 0, P), True, False)
        mm(pt, QZ, W256, False, True)
        act(("s6", 0, 256), (pt, 0, 256), AF.Sign, bias=0.5, acc=c1(SS + t))
        lin(c1(UU + t), c1(SS + t), 0.5, -129.0, "a")
        act(c1(MF + t), c1(EE), AF.Relu, bias=512.0, scale=-512.0)
        ts(("tgc", t, t + 1), c1(POS), c1(MF + t), c1(UU + t), OP.subtract, OP.max)
        dma("s", [(T.tg[t:t + 1, :], T.tgc[0:48, t:t + 1])], "tg%d" % t, regs(("tgc", t, t + 1)), [])

    for i in range(2):
        a, b = 128 * i, 128 * i + 128
        dma("s", [(T.oc[:, 4 * a:4 * b], T.ca3[:, a:b].bitcast(dt.uint8))], "outs", regs(("ca3", a, b)), [])
        mm("p%d" % (1 + 2 * i), ("qw", 0, 128), ("ca3", a, b))
    dma("a", [(T.osc[4 * k:4 * k + 4, 0:P], T.ca3s[32 * k:32 * k + 4, 0:P]) for k in range(4)], "osc", regs(("ca3s", 0, P)), [])
    lin(("yo", 0, 128), ("p1", 0, 128), None, None)
    lin(("yo", 128, 256), ("p3", 0, 128), None, None)
    for a in (0, 128):
        dma("s", [(T.y[:, a:a + 128], T.yo[:, a:a + 128])], "outs", regs(("yo", a, a + 128)), [])
    issue()
    g.wait_ge(T.sem.snd, snd[0])
    need("s", [("s" + e, count[e]) for e in "vatg"] + [(s, v) for s, v in total.items()])
